import numpy as np, ml_dtypes
CORES = [40,64,80,88,96,104,120,144]
N = 8
import mx_ref
BF = ml_dtypes.bfloat16
def f(rng, *shape):
    return mx_ref.flush((rng.standard_normal(shape, dtype=np.float32) * np.exp2(rng.integers(-2, 3, shape[:-1] + (1,)))).astype(BF))
def wide(rng, *shape, cols=0):
    v = rng.standard_normal(shape, dtype=np.float32) * np.exp2(rng.integers(-12, 13, shape)).astype(np.float32)
    if cols: v *= np.repeat(np.exp2(rng.integers(-cols, cols + 1, shape[:-2] + (1, shape[-1] // 4))) * (rng.random(shape[:-2] + (1, shape[-1] // 4)) > 0.0625), 4, axis=-1).astype(np.float32)
    return mx_ref.flush(v.astype(BF))
T, CAPP, O = 256, 64, 1
def scores(us, x):
    return mx_ref.matmul(mx_ref.quantize(us), mx_ref.quantize(x))[:8] + np.float32(0.0)
def winners(us, x):
    return np.argmax(np.stack([scores(us[s], x[s]) for s in range(N)]), axis=0)
def fill(rng, n, tot, most):
    n = np.array(n)
    while n.sum() < tot:
        q = rng.integers(0, N)
        if n[q] < most[q]: n[q] += 1
    return rng.permutation(np.repeat(np.arange(N), n))
def deal(rng, full):
    return np.stack([fill(rng, [CAPP if q in full[g] else 0 for q in range(N)], T, [CAPP] * N) for g in range(8)])
def one(rng):
    g, s = rng.integers(0, 8), rng.integers(0, N)
    return deal(rng, [[s] if i == g else [] for i in range(8)])
def heads(rng):
    u, h = np.zeros((8, 16, 128, 4), np.float32), np.arange(8)
    u[h, :, h] = rng.choice([-1.0, 1.0], (8, 16, 4)) * (0.25 + np.abs(rng.standard_normal((8, 16, 4)))) * np.exp2(rng.integers(-2, 3, (8, 16, 1)))
    return np.repeat(u.reshape(1, 128, 512).astype(BF), N, axis=0)
def plant(rng, x, us, wn, big=4, tie=None, zero=None):
    v = np.abs(x.astype(np.float32)).reshape(N, 8, 16, T, 4)
    v[v < 2.0 ** -24] = 0
    h, b = np.arange(8), np.float32(big)
    a = np.sign(us.astype(np.float32)).reshape(8, 16, 128, 4)[h, :, h][:, :, None]
    win = (wn == np.arange(N)[:, None, None])[:, :, None, :, None]
    neg = (rng.random((8, T)) < 0.125)[:, None, :, None]
    c = np.where(rng.random(v.shape, dtype=np.float32) < 0.5, np.float32(-1), np.float32(1))
    t = (np.where(neg, np.where(win, -a, -4 * b * a), np.where(win, b * a, c)) * v).astype(np.float32)
    s = np.stack([scores(us, t[r].reshape(128, 4 * T).astype(BF)) for r in range(N)])
    won = np.take_along_axis(s, wn[None], axis=0)[0]
    lost = np.where(win[:, :, 0, :, 0], -np.inf, s).max(axis=0)
    bad = (~(won - lost > 0.5 * np.abs(won)))[:, None, :, None]
    t = np.where(bad, np.where(win, b * a, -a) * v, t).astype(np.float32)
    if tie is not None:
        best = np.where(win, t, np.float32(0)).sum(axis=0)
        t = np.where(tie[:, None, :, None] & (wn < np.arange(N)[:, None, None])[:, :, None, :, None], best, t)
    if zero is not None: t[:, :, :, zero] = 0
    return t.reshape(N, 128, 4 * T).astype(BF)
def narrow(rng, x, us, wn):
    v, h = x.astype(np.float32).reshape(N, 8, 16, T, 4), np.arange(8)
    u = np.abs(us.astype(np.float32)).reshape(8, 16, 128, 4)[h, :, h]
    i, b = np.unravel_index(u.reshape(8, 64).argmin(axis=1), (16, 4))
    win = wn == np.arange(N)[:, None, None]
    part = np.where(win[:, :, None, :, None], v, np.float32(0)).sum(axis=0)
    p = np.exp2(np.floor(np.log2((u[:, :, None] * np.abs(part)).sum(axis=(1, 3))) - np.log2(u[h, i, b])[:, None]) - 12)
    z = np.stack([np.where(part[g, i[g], :, b[g]] < 0, -p[g], p[g]) for g in range(8)])
    close = np.repeat((rng.permutation(T) < T // 3)[None], 8, axis=0)
    other = (wn + rng.integers(1, N, (8, T))) % N
    hold = ((rng.random((N, 8, T)) < 0.25) | (other == np.arange(N)[:, None, None])) & ~win & close
    held = hold | (win & close)
    t = np.where(held[:, :, None, :, None], part, v).astype(np.float32)
    d = np.where(hold, rng.choice([-0.125, 0.125], (N, 8, T)), 0.0)
    for k in range(2):
        for g in range(8): t[:, g, i[g], :, b[g]] = np.where(held[:, g], z[g] * (1.5 + d[:, g]), t[:, g, i[g], :, b[g]])
        s = np.stack([scores(us, t[r].reshape(128, 4 * T).astype(BF)) for r in range(N)])
        if k == 0: d = np.where(s == np.take_along_axis(s, wn[None], axis=0), 2 * d, d)
    now = np.argmax(s, axis=0)
    for g in range(8):
        for k in range(T):
            n = np.bincount(now[g], minlength=N)
            q = n.argmax()
            if n[q] <= CAPP: break
            j = rng.permutation(np.flatnonzero((now[g] == q) & (wn[g] != q)))[:n[q] - CAPP]
            now[g, j] = wn[g, j]; close[g, j] = False
    return np.where(close[:, None, :, None], t, v).reshape(N, 128, 4 * T).astype(BF)
def draw(rng, wn, **k):
    us = heads(rng)
    return {"x": plant(rng, f(rng, N, 128, 4 * T), us[0], wn, **k), "us": us, "w": f(rng, N, 128, 512 * O)}
def setup_inputs(rng):
    return draw(rng, one(rng))
def setup_inputs_equal(rng):
    e, p = CAPP - 8, rng.permutation(T)
    far = np.stack([fill(rng, [8] + [0] * (N - 1), T - e, [8] + [CAPP] * (N - 1)) for g in range(8)])
    wn = np.concatenate([np.zeros((8, e), int), far], axis=1)[:, p]
    tie = np.repeat(np.concatenate([np.ones(e, bool), np.arange(T - e) % 2 == 0])[None], 8, axis=0)[:, p]
    return draw(rng, wn, tie=tie, zero=(np.arange(T) < 4)[p])
def setup_inputs_full(rng):
    s, k = int(rng.integers(0, N)), T // CAPP
    return draw(rng, deal(rng, [[s] + [q for q in rng.permutation(N).tolist() if q != s][:k - 1] for g in range(8)]))
def setup_inputs_near(rng):
    wn = one(rng)
    d = draw(rng, wn); d["x"] = narrow(rng, d["x"], d["us"][0], wn); return d
def setup_inputs_spread(rng):
    wn, us = one(rng), heads(rng)
    e = np.exp2(rng.integers(-4, 5, (N, 8, 1, T, 1))) * ((rng.random((N, 8, 1, T, 1)) > 0.0625) | (wn == np.arange(N)[:, None, None])[:, :, None, :, None])
    x = wide(rng, N, 128, 4 * T).astype(np.float32).reshape(N, 8, 16, T, 4) * e.astype(np.float32)
    return {"x": plant(rng, x, us[0], wn, big=256), "us": us, "w": f(rng, N, 128, 512 * O)}
def setup_inputs_stretch(rng):
    L = []
    for g in range(8):
        s, a = rng.integers(0, N), rng.choice([0, T - CAPP, rng.integers(0, T - CAPP + 1)])
        far = fill(rng, [0] * N, T - CAPP, [0 if q == s else CAPP for q in range(N)])
        L.append(np.concatenate([far[:a], np.full(CAPP, s), far[a:]]))
    return draw(rng, np.stack(L))
def check_inputs(d):
    b = []
    for k in ("x", "us", "w"):
        v = np.abs(np.asarray(d[k]).astype(np.float32))
        if not ((v == 0) | ((v >= 2.0 ** -30) & (v <= 2.0 ** 30))).all(): b.append(k)
    if b: return b
    u, h = np.array(d["us"]).astype(np.float32), np.arange(8)
    same = (u == u[:1]).all()
    u = u.reshape(N, 8, 16, 128, 4); u[:, h, :, h] = 0
    if not same or (u != 0).any(): b.append("us")
    wn = winners(d["us"], d["x"])
    if max((wn == s).sum(axis=1).max() for s in range(N)) > CAPP: b.append("x")
    return b
def reference(x, us, w):
    wn = winners(us, x)
    M = []
    for s in range(N):
        v = np.where((wn == s)[:, None, :, None], x[s].astype(np.float32).reshape(8, 16, T, 4), np.float32(0))
        M.append(mx_ref.quantize(np.ascontiguousarray(v.reshape(128, 4 * T).astype(BF))))
    y = np.zeros((N, 128, O * T), np.float32)
    for r in range(N):
        for o in range(O):
            W = mx_ref.quantize(np.ascontiguousarray(w[r][:, 512 * o:512 * o + 512]))
            for s in range(N): y[r][:, T * o:T * o + T] += mx_ref.matmul(W, M[s])
    return {"y": y, "wn": np.repeat(wn.astype(np.float32)[None], N, axis=0)}

@@ -1,0 +1,368 @@
+from concourse.bass import DstId, RemoteDMATransfer
+from concourse.mybir import dt, AluOpType as A, ActivationFunctionType
+
+N = 8
+CODES = "float8_e4m3fn_x4"
+ROW = 80
+WIN = 17 * ROW
+FIRST = 3
+
+
+def sb(kind, **cols):
+    return {k: ("sbuf", [128, n], kind) for k, n in cols.items()}
+
+
+SCRATCH = {"ps": ("psum", [128, 4096], "float32")}
+SCRATCH.update(sb("bfloat16", xb=1024, usl=32, zb=560, pk=512, wz=4096, zz=512))
+SCRATCH.update(sb(CODES, zq=140, xq=384, wq=1024, oq=128, pq=512, rq=64))
+SCRATCH.update(sb("uint8", zp=140, xp=384, wp=1024, op=128, pp=512, rp=64))
+SCRATCH.update(sb("int32", pi=1, pj=4))
+SCRATCH.update(sb("float32", pf=4, c64=64, d64=64, m4=64, msk=64, mk2=64, v0=256, val=256, pc0=16, pc=16, qr=1, one=16,
+                  rm=128, k8=8, prio=128, rc=8))
+SCRATCH.update(sb("float32", rsc=16, sm=64, s32=32, sc=128, repa=64, repb=64, la=64, la2=32, la3=16, pen=16, cb=64, cb2=32,
+                  lose=16, tb=32, tt=32, ts=32, bt=32, lp=16, fo=16, inv=WIN, mkd=64, sel=64))
+SCRATCH.update(sb("uint16", offa=16, offb=16, off=128))
+SCRATCH.update(sb("float32", m64=64, m32=32, m16=32, eq=128, eqp=128, e64=64, e32=32, pv=32, wnv=16, win=128, win2=128, cum=128,
+                  t2=128, ts2=128, b2=128, bk=8, cu2=128, pr=128, f64=64, f32=32, x1=32, t1=64, res=4096, ya=256, yb=256))
+SEMAPHORES = (["cv", "cw", "loc", "scA", "scB", "cqA", "cqB", "rs0", "rs1", "rs2", "kc",
+               "lus", "lx", "lw0", "lw1", "lown", "lwn", "ly",
+               "kz", "kzz", "kzs", "kzq", "kxp", "kxq", "ksc", "ksr", "kps", "kpsr", "kio", "kio0", "kpf", "kpz", "kval",
+               "kpr", "kw0", "kw1", "kwq0", "kwq1",
+               "kpk", "kwn", "kwin", "kw2", "ky0", "ky1"] + ["%s%d" % (k, h) for k in ("ma", "da", "mb", "db") for h in range(8)])
+
+
+def order(T, topo):
+    a = [c for c in T.cores if c == T.cores[0] or topo.may_write(T.cores[0], c)]
+    return [a, [c for c in T.cores if c not in a]]
+
+
+def roads(core, T, topo):
+    two = order(T, topo)
+    own, far = two if core in two[0] else two[::-1]
+    near = [c for c in own if c != core]
+    cand = [c for c in topo.cores_of(core) if c not in T.cores and all(topo.may_write(c, d) for d in far)]
+    a = [c for c in cand if topo.die(c) != topo.die(core)]
+    b = [c for c in cand if topo.die(c) == topo.die(core)]
+    hc, hp = [a[0], b[0]], [a[1], b[1]]
+    k = own.index(core)
+    codes = {h: [d for j, d in enumerate(far) if (j + k) % 2 == i] for i, h in enumerate(hc)}
+    planes = {h: [d for j, d in enumerate(far) if (j + k) % 2 == i] for i, h in enumerate(hp)}
+    nplanes = dict(zip(hc + [hp[k % 2]], [[d] for d in near]))
+    scores = {h: [d for j, d in enumerate(far) if (j + k) % 4 == i] for i, h in enumerate(hc + hp)}
+    return {"near": near, "far": far, "codes": codes, "planes": planes, "nplanes": nplanes, "scores": scores,
+            "handed": hp + [h for h in hc if h in nplanes]}
+
+
+def bits(engines):
+    return sum(1 << e for e in engines)
+
+
+def write(g, core, dests, engines, src, dst, sem, T, topo):
+    i = []
+    for d in dests:
+        rid, pid = topo.addr(d, core)
+        i.append(DstId(rid=rid, pnc=pid))
+    g.remote_dma_fused([RemoteDMATransfer(dst_ids=i, dma_engine_mask=bits(engines), remote_sem=T.sem[sem],
+                                          srcs=[src], dsts=[dst] * len(i))], local_sem=T.sem.loc)
+    return len(engines)
+
+
+def engines_of(core, near, helper, topo):
+    off, every = topo.engines(core, near), topo.engines(core, helper)
+    return off, [e for e in every if e not in off], every
+
+
+def relay(g, core, boss, T, topo):
+    r = roads(boss, T, topo)
+    if core not in r["scores"]:
+        return
+    p = sum(order(T, topo), []).index(boss)
+    eng = topo.engines(core, r["far"][0])
+    _, eon, every = engines_of(boss, r["near"][0], core, topo)
+    half, what = list(r["scores"]).index(core) % 2, list(r["scores"]).index(core) // 2
+    step, base, buf = ((0, 1, T.one), (1, 8 * half, T.pc0))[what]
+    g.iota(T.rc[:], [[step, 8]], base, 0, allow_small_or_imprecise_dtypes=True).then_inc(T.sem.kio, 1)
+    g.wait_ge(T.sem.kio, 1)
+    n = write(g, core, [boss], eng, T.rc[:], buf[:, 8 * half:8 * half + 8], "kc", T, topo)
+    g.wait_ge(T.sem.rs0, len(eon))
+    n += write(g, core, r["scores"][core], eng, T.rsc[:], T.sc[:, 16 * p:16 * p + 16], "scB", T, topo)
+    if core in r["codes"]:
+        g.wait_ge(T.sem.rs1, len(every))
+        n += write(g, core, r["codes"][core], eng, T.rq[:].bitcast(dt.uint8), T.pq[:, 64 * p:64 * p + 64].bitcast(dt.uint8),
+                   "cqB", T, topo)
+    if core in r["handed"]:
+        g.wait_ge(T.sem.rs2, len(every))
+    for road, sem in (("planes", "cqB"), ("nplanes", "cqA")):
+        if core in r[road]:
+            n += write(g, core, r[road][core], eng, T.rp[:], T.pp[:, 64 * p:64 * p + 64], sem, T, topo)
+    g.wait_ge(T.sem.loc, n)
+
+
+def rank_program(g, core, T, topo):
+    rank = T.rank_of(core)
+    if rank is None:
+        for boss in T.cores:
+            if core in topo.cores_of(boss):
+                relay(g, core, boss, T, topo)
+        return
+    road = roads(core, T, topo)
+    near, far = road["near"], road["far"]
+    two = order(T, topo)
+    pieces = two[0] + two[1]
+    cls = 0 if core in two[0] else 1
+    mine = pieces.index(core)
+    idx = two[cls].index(core)
+    rk = [T.rank_of(c) for c in pieces]
+
+    Q = {"v": [g.vector, "cv"], "s": [g.scalar, None], "t": [g.tensor, None], "g": [g, None], "y": [g.sync, None]}
+    total = {}
+    seen = {q: {} for q in Q}
+
+    def wait(q, *deps):
+        for d in deps:
+            if d is None:
+                continue
+            sem, val = d
+            if sem in ("cv", "cw"):
+                val = total[sem]
+            if seen[q].get(sem, 0) < val:
+                Q[q][0].wait_ge(T.sem[sem], val)
+                seen[q][sem] = val
+
+    def run(q, ins, key=None, n=1):
+        sem = key or Q[q][1]
+        ins.then_inc(T.sem[sem], n)
+        total[sem] = total.get(sem, 0) + n
+        return (sem, total[sem])
+
+    def V(name, *args, deps=(), key=None):
+        wait("v", *deps)
+        f = {"set": g.vector.memset, "cp": g.vector.tensor_copy, "tt": g.vector.tensor_tensor, "ts": g.vector.tensor_scalar,
+             "scan": g.vector.tensor_tensor_scan, "tr": g.vector.transpose, "q": g.vector.quantize_mx}[name]
+        return run("v", f(*args), key)
+
+    def S(out, in_, deps=(), key=None, **line):
+        wait("s", *deps)
+        return run("s", g.scalar.activation(out, in_, ActivationFunctionType.Identity if line else ActivationFunctionType.Copy, **line), key)
+
+    def iota(out, pattern, base, cm, key="kio"):
+        return run("g", g.iota(out, pattern, base, cm, allow_small_or_imprecise_dtypes=True), key)
+
+    lus = run("y", g.sync.dma_start(T.usl[:], T.us[:, 0:32]), "lus", 16)
+    lx = run("s", g.scalar.dma_start(T.xb[:], T.x[:]), "lx", 16)
+
+    iota(T.pi[:], [[0, 1]], 0, 1, "kio0")
+    kio0 = iota(T.c64[:], [[1, 4], [0, 16]], 0, 0, "kio0")
+    iota(T.d64[:], [[0, 16], [1, 4]], 0, 0)
+    iota(T.k8[:], [[64, 8]], -1, 0)
+    kio = iota(T.v0[:], [[4, 16], [64, 16]], 0, 0)
+
+    kzz = V("set", T.zz[:], 0.0, key="kzz")
+    kz = V("set", T.zb[:], 0.0, key="kz")
+    kxp = V("q", T.xq[:, 256:384], T.xp[:, 256:384], T.zz[:], deps=[kzz], key="kxp")
+
+    def zero(block, key):
+        return S(T.wz[:, 512 * block:512 * block + 512], T.zz[:], deps=[kzz], key=key)
+    zero(0, "kw0")
+    zero(1, "kw0")
+    zs = ksz = None
+    for l in range(4):
+        for e in range(4):
+            a = 4 * (12 + l) + e
+            o, i = T.zb[:, a:a + 449:64], T.usl[:, e:32:4]
+            if l < 2:
+                zs = V("cp", o, i, deps=[kz, lus])
+            else:
+                ksz = S(o, i, deps=[kz, lus], key="kzs")
+    kzq = V("q", T.zq[:], T.zp[:], T.zb[:], deps=[zs, ksz], key="kzq")
+    kxq = V("q", T.xq[:, 0:256], T.xp[:, 0:256], T.xb[:], deps=[lx], key="kxq")
+    zero(2, "kw0")
+    kw0 = zero(3, "kw0")
+    zero(4, "kw1")
+    zero(5, "kw1")
+    wait("v", kio0)
+    V("ts", T.pj[:, 0:1], T.pi[:], 3, None, A.bitwise_and)
+    V("ts", T.pj[:, 1:2], T.pi[:], 2, 3, A.arith_shift_right, A.bitwise_and)
+    t = V("ts", T.pj[:, 2:3], T.pi[:], 15, None, A.bitwise_and)
+    kpf = V("cp", T.pf[:, 0:3], T.pj[:, 0:3], deps=[t], key="kpf")
+    pt, pa, pqq = T.pf[:, 0:1], T.pf[:, 1:2], T.pf[:, 2:3]
+    tm = V("ts", T.msk[:], T.c64[:], pt, None, A.is_equal, deps=[kpf])
+
+    wait("t", kzq, kxp, kxq)
+    for i in range(4):
+        m = g.tensor.matmul_mx(T.ps[:, 0:128], T.zq[:, 12 - 4 * i:140 - 4 * i], T.zp[:, 12 - 4 * i:140 - 4 * i],
+                               T.xq[:, 64 * i:64 * i + 128], T.xp[:, 64 * i:64 * i + 128], i == 0, i == 3)
+    kps = run("t", m, "kps")
+    kpsr = V("tt", T.sm[:], T.ps[:, 0:64], T.msk[:], A.mult, deps=[kps, tm], key="kpsr")
+    t = V("tt", T.s32[:], T.sm[:, 0:32], T.sm[:, 32:64], A.add, deps=[kpsr])
+    own = T.sc[:, 16 * mine:16 * mine + 16]
+    ksc = V("tt", own, T.s32[:, 0:16], T.s32[:, 16:32], A.add, deps=[t], key="ksc")
+
+    hs = list(road["scores"])
+    eoff, eon, every = engines_of(core, near[0], hs[0], topo)
+    nA = len(near) * len(eoff)
+    theirs = {c: roads(c, T, topo) for c in near + far}
+
+    def arriving(c, *kinds):
+        return sum(len(topo.engines(h, core)) for k in kinds for h, d in theirs[c][k].items() if core in d)
+    nB = sum(arriving(c, "scores") for c in far)
+    kc = ("kc", sum(len(topo.engines(h, far[0])) for h in hs))
+    wait("g", ksc)
+    loc = write(g, core, hs, eon, own, T.rsc[:], "rs0", T, topo)
+    loc += write(g, core, near, eoff, own, own, "scA", T, topo)
+
+    ksr = None
+    for i in range(4):
+        ksr = S(T.repa[:, 16 * i:16 * i + 16], own, deps=[ksc], key="ksr")
+    kpz = S(T.pk[:, 256:512], T.zz[:, 0:256], deps=[kzz], key="kpz")
+    zero(6, "kw1")
+    kw1 = zero(7, "kw1")
+    t = V("set", T.rm[:], 1.0)
+    V("set", T.la[:, 16 * idx:16 * idx + 16], 0.0)
+    V("set", T.tb[:], 0.0)
+    V("set", T.ts[:], 0.0)
+    V("set", T.ts2[:, 0:1], 0.0)
+    V("set", T.inv[:, 0:64], 0.0)
+    V("set", T.rm[:, 0:128:16], 0.0, deps=[t])
+    kval = S(T.val[:], T.v0[:], deps=[kio, kpf], key="kval", bias=pt)
+    for i in range(8):
+        kpr = S(T.prio[:, 16 * i:16 * i + 16], T.one[:], deps=[kc], key="kpr", scale=float(8 - rk[i]))
+    for half, kw in enumerate((kw0, kw1)):
+        wait("y", kw)
+        for h in range(4 * half, 4 * half + 4):
+            run("y", g.sync.dma_start(T.wz[16 * h:16 * h + 16, 512 * h:512 * h + 512], T.w[16 * h:16 * h + 16, :]), "lw%d" % half, 16)
+
+    def wquant(half):
+        V("q", T.wq[:, 512 * half:512 * half + 512], T.wp[:, 512 * half:512 * half + 512],
+          T.wz[:, 2048 * half:2048 * half + 2048], deps=[("lw%d" % half, 64)], key="kwq%d" % half)
+    wait("v", kio)
+    V("ts", T.m4[:], T.d64[:], 1.0, None, A.min)
+    V("ts", T.mk2[:], T.d64[:], pa, None, A.is_equal)
+    t = V("ts", T.qr[:], pqq, float(ROW), float(ROW + 1), A.mult, A.add)
+    wquant(0)
+    V("ts", T.pc[:], T.pc0[:], T.qr[:], None, A.add, deps=[t, kc])
+
+    ca, cb = 64 * cls, 64 * (1 - cls)
+    wait("v", ksr, ("scA", nA), ksc)
+    a = 16 * idx
+    if idx > 0:
+        t = V("tt", T.la[:, 0:a], T.sc[:, ca:ca + a], T.repa[:, 0:a], A.is_ge)
+    if idx < 3:
+        t = V("tt", T.la[:, a + 16:64], T.sc[:, ca + a + 16:ca + 64], T.repa[:, a + 16:64], A.is_gt)
+    t = V("tt", T.la2[:], T.la[:, 0:32], T.la[:, 32:64], A.max, deps=[t])
+    t = V("tt", T.la3[:], T.la2[:, 0:16], T.la2[:, 16:32], A.max, deps=[t])
+    t = V("ts", T.pen[:], T.la3[:], -1e28, None, A.mult, deps=[t])
+    for i in range(4):
+        tr = V("tt", T.repb[:, 16 * i:16 * i + 16], own, T.pen[:], A.add, deps=[t] if i == 0 else [])
+    wquant(1)
+
+    wait("v", tr, ("scB", nB))
+    low = 16 * len([c for c in far if T.rank_of(c) < rank])
+    if low > 0:
+        t = V("tt", T.cb[:, 0:low], T.sc[:, cb:cb + low], T.repb[:, 0:low], A.is_ge)
+    if low < 64:
+        t = V("tt", T.cb[:, low:64], T.sc[:, cb + low:cb + 64], T.repb[:, low:64], A.is_gt)
+    t = V("tt", T.cb2[:], T.cb[:, 0:32], T.cb[:, 32:64], A.max, deps=[t])
+    t = V("tt", T.lose[:], T.cb2[:, 0:16], T.cb2[:, 16:32], A.max, deps=[t])
+    t = V("scan", T.tb[:, 0:16], T.one[:], T.lose[:], -1.0, A.add, A.subtract, deps=[t, kc])
+    tw = V("tt", T.lp[:], T.lose[:], T.pc[:], A.mult, key="cw")
+    t = V("tr", T.tt[:], T.tb[:], deps=[t])
+    tw = V("tt", T.fo[:], T.tb[:, 0:16], T.lp[:], A.add, deps=[tw], key="cw")
+    t = V("scan", T.ts[:, 1:32], T.tt[:, 0:31], T.rm[:, 1:32], 0.0, A.add, A.mult, deps=[t])
+    t = V("tr", T.bt[:], T.ts[:], deps=[t])
+    t = V("ts", T.offa[:], T.fo[:], T.bt[:, 15:16], pqq, A.add, A.add, deps=[t, tw, kpf])
+    t = V("cp", T.inv[:, 0:WIN].indirect(T.offa[:, 0:16]), T.val[:], deps=[t, kval])
+    t = V("tt", T.mkd[:], T.inv[:, 0:64], T.mk2[:], A.mult, deps=[t])
+    t = V("scan", T.sel[:], T.m4[:], T.mkd[:], 0.0, A.mult, A.add, deps=[t])
+    t = V("cp", T.offb[:], T.sel[:, 3:64:4], deps=[t])
+    t = V("cp", T.pk[:, 0:256], T.xb[:, 0:1024].indirect(T.offb[:, 0:16]), deps=[t])
+    kpk = V("q", T.oq[:], T.op[:], T.pk[:], deps=[t, kpz], key="kpk")
+
+    c0 = 64 * mine
+    oq, pq = T.oq[:, 0:64].bitcast(dt.uint8), T.pq[:, c0:c0 + 64].bitcast(dt.uint8)
+    op, pp = T.op[:, 0:64], T.pp[:, c0:c0 + 64]
+    wait("g", kpk)
+    loc += write(g, core, list(road["codes"]), every, oq, T.rq[:].bitcast(dt.uint8), "rs1", T, topo)
+    loc += write(g, core, road["handed"], every, op, T.rp[:], "rs2", T, topo)
+    loc += write(g, core, near, eoff, oq, pq, "cqA", T, topo)
+    wait("y", kpk)
+    run("y", g.sync.dma_start(pq, oq), "lown", 16)
+    run("y", g.sync.dma_start(pp, op), "lown", 16)
+
+    t = V("tt", T.m64[:], T.sc[:, 0:64], T.sc[:, 64:128], A.max)
+    t = V("tt", T.m32[:], T.m64[:, 0:32], T.m64[:, 32:64], A.max, deps=[t])
+    for i in range(2):
+        tm = V("tt", T.m16[:, 16 * i:16 * i + 16], T.m32[:, 0:16], T.m32[:, 16:32], A.max, deps=[t] if i == 0 else [])
+    for i in range(4):
+        t = V("tt", T.eq[:, 32 * i:32 * i + 32], T.sc[:, 32 * i:32 * i + 32], T.m16[:], A.is_equal, deps=[tm] if i == 0 else [])
+    t = V("tt", T.eqp[:], T.eq[:], T.prio[:], A.mult, deps=[t, kpr])
+    t = V("tt", T.e64[:], T.eqp[:, 0:64], T.eqp[:, 64:128], A.max, deps=[t])
+    t = V("tt", T.e32[:], T.e64[:, 0:32], T.e64[:, 32:64], A.max, deps=[t])
+    for i in range(2):
+        tm = V("tt", T.pv[:, 16 * i:16 * i + 16], T.e32[:, 0:16], T.e32[:, 16:32], A.max, deps=[t] if i == 0 else [])
+    for i in range(4):
+        kwin = V("tt", T.win[:, 32 * i:32 * i + 32], T.pv[:], T.prio[:, 32 * i:32 * i + 32], A.is_equal,
+                 deps=[tm] if i == 0 else [], key="kwin")
+    kw2 = S(T.win2[:], T.win[:], deps=[kwin], key="kw2")
+    kwn = S(T.wnv[:], T.pv[:, 0:16], deps=[kwin], key="kwn", scale=-1.0, bias=8.0)
+    t = V("scan", T.cum[:], T.rm[:], T.win[:], 0.0, A.mult, A.add, deps=[kwin])
+    t = V("tr", T.t2[:], T.cum[:], deps=[t])
+    t = V("scan", T.ts2[:, 1:128], T.t2[:, 0:127], T.rm[:, 1:128], 0.0, A.add, A.mult, deps=[t])
+    t = V("tr", T.b2[:], T.ts2[:], deps=[t])
+    t = V("tt", T.bk[:], T.b2[:, 15:128:16], T.k8[:], A.add, deps=[t])
+    t = V("tt", T.win2[:, 0:128:16], T.win2[:, 0:128:16], T.bk[:], A.add, deps=[t, kw2])
+    t = V("scan", T.cu2[:], T.rm[:], T.win2[:], 0.0, A.mult, A.add, deps=[t])
+    t = V("tt", T.pr[:], T.cu2[:], T.win[:], A.mult, deps=[t])
+    t = V("tt", T.f64[:], T.pr[:, 0:64], T.pr[:, 64:128], A.add, deps=[t])
+    t = V("tt", T.f32[:], T.f64[:, 0:32], T.f64[:, 32:64], A.add, deps=[t])
+    V("tt", T.x1[:, 0:16], T.f32[:, 0:16], T.f32[:, 16:32], A.add, deps=[t])
+    t = V("tt", T.x1[:, 16:32], T.f32[:, 0:16], T.f32[:, 16:32], A.add)
+    V("tr", T.t1[0:64, 0:32], T.x1[0:64, :], deps=[t])
+    t = V("tr", T.t1[64:128, 32:64], T.x1[64:128, :])
+    V("cp", T.t1[64:128, 0:32], T.t1[0:64, 0:32], deps=[t])
+    t = V("cp", T.t1[0:64, 32:64], T.t1[64:128, 32:64])
+    for e in range(2):
+        for b in range(4):
+            a = b // 2 * 2 + e
+            t = V("cp", T.off[32 * b:32 * b + 32, 64 * e:64 * e + 64], T.t1[32 * a:32 * a + 32, 0:64], deps=[t] if e + b == 0 else [])
+    toff = t
+    wait("y", kwn)
+    run("y", g.sync.dma_start(T.wn[:], T.wnv[:]), "lwn", 16)
+
+    def product(h, half, bank, key, deps):
+        wait("t", *deps)
+        return run("t", g.tensor.matmul_mx(T.ps[:, 512 * bank:512 * bank + 256], T.wq[:, 128 * h:128 * h + 128], T.wp[:, 128 * h:128 * h + 128],
+                                           T.pq[:, 256 * half:256 * half + 256], T.pp[:, 256 * half:256 * half + 256], True, True), key)
+
+    def drain(h, half, bank, key, k):
+        o = 512 * h + 256 * half
+        return S(T.res[:, o:o + 256], T.ps[:, 512 * bank:512 * bank + 256], deps=[k], key=key)
+    da, db = {}, {}
+    wait("t", ("kwq0", 1), ("kwq1", 1), kpsr, ("cqB", sum(arriving(c, "codes", "planes") for c in far)))
+    mb = [product(h, 1 - cls, h, "mb%d" % h, []) for h in range(8)]
+    for h in range(FIRST):
+        db[h] = drain(h, 1 - cls, h, "db%d" % h, mb[h])
+    wait("t", ("lown", 32), ("cqA", sum(len(eoff) + arriving(c, "nplanes") for c in near)))
+    for h in range(8):
+        bank = h % FIRST
+        if h >= FIRST:
+            db[h] = drain(h, 1 - cls, h, "db%d" % h, mb[h])
+        da[h] = drain(h, cls, bank, "da%d" % h, product(h, cls, bank, "ma%d" % h, [db[h] if h < FIRST else da[h - FIRST]]))
+
+    def found(h, a, b):
+        o = 64 * (h // 2 % 2) + 32 * (h // 4) + 16 * (h % 2)
+        return T.res[:, 512 * h:512 * h + 512].indirect(T.off[:, o + a // 16:o + b // 16])
+    out, prev = T.ya, T.yb
+    acc = V("cp", out[:], found(0, 0, 256), deps=[toff, da[0], db[0]])
+    for h in range(1, 7):
+        out, prev = prev, out
+        acc = V("tt", out[:], found(h, 0, 256), prev[:], A.add, deps=[acc, da[h], db[h]])
+    out, prev = prev, out
+    for i, q in enumerate(("y", "s")):
+        a, b = 128 * i, 128 * i + 128
+        k = V("tt", out[:, a:b], found(7, a, b), prev[:, a:b], A.add, deps=[acc, da[7], db[7]], key="ky%d" % i)
+        wait(q, k)
+        run(q, Q[q][0].dma_start(T.y[:, a:b], out[:, a:b]), "ly", 16)
+
+    wait("g", ("ly", 32), ("lwn", 16), ("loc", loc))
+    g.wait_ge(T.sem.cv, total["cv"])

@@ -4,8 +4,8 @@ from concourse.mybir import dt, AluOpType as A, ActivationFunctionType
 N = 8
 CODES = "float8_e4m3fn_x4"
 ROW = 80
-WIN = 17 * ROW
-FIRST = 3
+WIN = 129 * ROW
+OWN = 64 * (N - 1)
 
 
 def sb(kind, **cols):
@@ -13,21 +13,22 @@ def sb(kind, **cols):
 
 
 SCRATCH = {"ps": ("psum", [128, 4096], "float32")}
-SCRATCH.update(sb("bfloat16", xb=1024, usl=32, zb=560, pk=512, wz=4096, zz=512))
-SCRATCH.update(sb(CODES, zq=140, xq=384, wq=1024, oq=128, pq=512, rq=64))
-SCRATCH.update(sb("uint8", zp=140, xp=384, wp=1024, op=128, pp=512, rp=64))
-SCRATCH.update(sb("int32", pi=1, pj=4))
-SCRATCH.update(sb("float32", pf=4, c64=64, d64=64, m4=64, msk=64, mk2=64, v0=256, val=256, pc0=16, pc=16, qr=1, one=16,
-                  rm=128, k8=8, prio=128, rc=8))
+SCRATCH.update(sb("bfloat16", xb=1024, usl=32, u16=16, zb=560, pk=512, wz=4096, zz=512))
+SCRATCH.update(sb(CODES, zq=140, xq=384, wq=1024, pq=576, rq=64))
+SCRATCH.update(sb("uint8", zp=140, xp=384, wp=1024, pp=576, rp=64))
+SCRATCH.update(sb("int32", pi=1, pj=4, wi=16))
+SCRATCH.update(sb("float32", pf=4, p4=1, c64=64, d64=64, msk=64, val=256, pc=16, one=16, k8=8))
+SCRATCH.update(sb("bfloat16", rm=128, a4=64))
 SCRATCH.update(sb("float32", rsc=16, sm=64, s32=32, sc=128, repa=64, repb=64, la=64, la2=32, la3=16, pen=16, cb=64, cb2=32,
-                  lose=16, tb=32, tt=32, ts=32, bt=32, lp=16, fo=16, inv=WIN, mkd=64, sel=64))
-SCRATCH.update(sb("uint16", offa=16, offb=16, off=128))
-SCRATCH.update(sb("float32", m64=64, m32=32, m16=32, eq=128, eqp=128, e64=64, e32=32, pv=32, wnv=16, win=128, win2=128, cum=128,
-                  t2=128, ts2=128, b2=128, bk=8, cu2=128, pr=128, f64=64, f32=32, x1=32, t1=64, res=4096, ya=256, yb=256))
-SEMAPHORES = (["cv", "cw", "loc", "scA", "scB", "cqA", "cqB", "rs0", "rs1", "rs2", "kc",
-               "lus", "lx", "lw0", "lw1", "lown", "lwn", "ly",
-               "kz", "kzz", "kzs", "kzq", "kxp", "kxq", "ksc", "ksr", "kps", "kpsr", "kio", "kio0", "kpf", "kpz", "kval",
-               "kpr", "kw0", "kw1", "kwq0", "kwq1",
+                  lose=16, tb=32, tt=32, ts=32, bt=32, lp=16, fo=16, inv=WIN, sel=64))
+SCRATCH.update(sb("uint16", uo=4, offa=16, offb=16, off=128))
+SCRATCH.update(sb("bfloat16", win=128, cum=128, t2=128, ts2=128, b2=128))
+SCRATCH.update(sb("float32", st=128, g1=64, m1=64, g2=32, m2=32, w3=32, w2=64, win2=128, cu2=128, pr=128, f64=64, f32=32,
+                  x1=32, t1=64, fr=16, wnv=16, res=4096, ya=256, yb=256))
+SEMAPHORES = (["cv", "cw", "loc", "scA", "scB", "cq", "rs0", "rs1", "rs2", "kc",
+               "lus", "lx", "lw0", "lw1", "lwn", "ly",
+               "kz", "kzz", "kzq", "kxp", "kxq", "ksc", "ksr", "kps", "kpsr", "kio", "kio0", "kpz", "kst", "kob", "kg",
+               "kw0", "kw1", "kw7", "kwq0", "kwq1", "kfr", "md", "dd",
                "kpk", "kwn", "kwin", "kw2", "ky0", "ky1"] + ["%s%d" % (k, h) for k in ("ma", "da", "mb", "db") for h in range(8)])
 
 
@@ -40,30 +41,38 @@ def roads(core, T, topo):
     two = order(T, topo)
     own, far = two if core in two[0] else two[::-1]
     near = [c for c in own if c != core]
-    cand = [c for c in topo.cores_of(core) if c not in T.cores and all(topo.may_write(c, d) for d in far)]
+    free = [c for c in topo.cores_of(core) if c not in T.cores]
+    cand = [c for c in free if all(topo.may_write(c, d) for d in far)]
     a = [c for c in cand if topo.die(c) != topo.die(core)]
     b = [c for c in cand if topo.die(c) == topo.die(core)]
+    rest = [c for c in free if c not in cand and topo.die(c) != topo.die(core)]
     hc, hp = [a[0], b[0]], [a[1], b[1]]
     k = own.index(core)
     codes = {h: [d for j, d in enumerate(far) if (j + k) % 2 == i] for i, h in enumerate(hc)}
     planes = {h: [d for j, d in enumerate(far) if (j + k) % 2 == i] for i, h in enumerate(hp)}
-    nplanes = dict(zip(hc + [hp[k % 2]], [[d] for d in near]))
-    scores = {h: [d for j, d in enumerate(far) if (j + k) % 4 == i] for i, h in enumerate(hc + hp)}
-    return {"near": near, "far": far, "codes": codes, "planes": planes, "nplanes": nplanes, "scores": scores,
-            "handed": hp + [h for h in hc if h in nplanes]}
+    planes.update({rest[0]: near[:2], rest[1]: near[2:]})
+    return {"near": near, "far": far, "codes": codes, "planes": planes, "scores": codes, "helpers": list(codes) + list(planes)}
+
+
+def column(src, dst, T):
+    return 64 * ((T.rank_of(src) - T.rank_of(dst) - 1) % N)
+
+
+def seat(k):
+    return 4 * (k % 2) + 2 * (k // 2 % 2) + k // 4
 
 
 def bits(engines):
     return sum(1 << e for e in engines)
 
 
-def write(g, core, dests, engines, src, dst, sem, T, topo):
+def write(g, core, dests, engines, src, dsts, sem, T, topo):
     i = []
     for d in dests:
         rid, pid = topo.addr(d, core)
         i.append(DstId(rid=rid, pnc=pid))
     g.remote_dma_fused([RemoteDMATransfer(dst_ids=i, dma_engine_mask=bits(engines), remote_sem=T.sem[sem],
-                                          srcs=[src], dsts=[dst] * len(i))], local_sem=T.sem.loc)
+                                          srcs=[src], dsts=dsts)], local_sem=T.sem.loc)
     return len(engines)
 
 
@@ -72,29 +81,61 @@ def engines_of(core, near, helper, topo):
     return off, [e for e in every if e not in off], every
 
 
+def whole(g, out, pattern, base, cm, sem):
+    g.iota(out, pattern, base, cm, allow_small_or_imprecise_dtypes=True).then_inc(sem, 1)
+
+
+def constant(g, which, boss, T):
+    v, kio, cv = g.vector, T.sem.kio, T.sem.cv
+    if which < 2:
+        out = T.one[:, 8 * which:8 * which + 8]
+        whole(g, out, [[0, 8]], 1, 0, kio)
+    elif which < 4:
+        a = 8 * (which - 2)
+        out = T.pc[:, a:a + 8]
+        whole(g, out, [[1, 8]], ROW + 1 + a, ROW, kio)
+    elif which == 4:
+        out = T.k8[:]
+        for k in range(N):
+            v.memset(T.k8[:, k:k + 1], column(T.cores[seat(k)], boss, T) - 1 + seat(k) / 16).then_inc(kio, 1)
+        g.wait_ge(kio, N)
+        return out
+    else:
+        out = T.a4[:]
+        whole(g, T.pi[:], [[0, 1]], 0, 1, cv)
+        whole(g, T.d64[:], [[0, 16], [1, 4]], 0, 0, cv)
+        v.wait_ge(cv, 2)
+        v.tensor_scalar(T.pj[:, 0:1], T.pi[:], 2, 3, A.arith_shift_right, A.bitwise_and).then_inc(cv, 1)
+        v.wait_ge(cv, 3)
+        v.tensor_copy(T.pf[:, 0:1], T.pj[:, 0:1]).then_inc(cv, 1)
+        v.wait_ge(cv, 4)
+        v.tensor_scalar(out, T.d64[:], T.pf[:, 0:1], 2048.0, A.is_equal, A.mult).then_inc(kio, 1)
+    g.wait_ge(kio, 1)
+    return out
+
+
 def relay(g, core, boss, T, topo):
     r = roads(boss, T, topo)
-    if core not in r["scores"]:
+    if core not in r["helpers"]:
         return
     p = sum(order(T, topo), []).index(boss)
-    eng = topo.engines(core, r["far"][0])
+    eng = topo.engines(core, r["near"][0])
     _, eon, every = engines_of(boss, r["near"][0], core, topo)
-    half, what = list(r["scores"]).index(core) % 2, list(r["scores"]).index(core) // 2
-    step, base, buf = ((0, 1, T.one), (1, 8 * half, T.pc0))[what]
-    g.iota(T.rc[:], [[step, 8]], base, 0, allow_small_or_imprecise_dtypes=True).then_inc(T.sem.kio, 1)
-    g.wait_ge(T.sem.kio, 1)
-    n = write(g, core, [boss], eng, T.rc[:], buf[:, 8 * half:8 * half + 8], "kc", T, topo)
-    g.wait_ge(T.sem.rs0, len(eon))
-    n += write(g, core, r["scores"][core], eng, T.rsc[:], T.sc[:, 16 * p:16 * p + 16], "scB", T, topo)
+    c = constant(g, r["helpers"].index(core), boss, T)
+    n = write(g, core, [boss], eng, c, [c], "kc", T, topo)
+    if core in r["scores"]:
+        g.wait_ge(T.sem.rs0, len(eon))
+        d = r["scores"][core]
+        n += write(g, core, d, eng, T.rsc[:], [T.sc[:, 16 * p:16 * p + 16]] * len(d), "scB", T, topo)
     if core in r["codes"]:
         g.wait_ge(T.sem.rs1, len(every))
-        n += write(g, core, r["codes"][core], eng, T.rq[:].bitcast(dt.uint8), T.pq[:, 64 * p:64 * p + 64].bitcast(dt.uint8),
-                   "cqB", T, topo)
-    if core in r["handed"]:
+        d = r["codes"][core]
+        to = [T.pq[:, column(boss, e, T):column(boss, e, T) + 64].bitcast(dt.uint8) for e in d]
+        n += write(g, core, d, eng, T.rq[:].bitcast(dt.uint8), to, "cq", T, topo)
+    else:
         g.wait_ge(T.sem.rs2, len(every))
-    for road, sem in (("planes", "cqB"), ("nplanes", "cqA")):
-        if core in r[road]:
-            n += write(g, core, r[road][core], eng, T.rp[:], T.pp[:, 64 * p:64 * p + 64], sem, T, topo)
+        d = r["planes"][core]
+        n += write(g, core, d, eng, T.rp[:], [T.pp[:, column(boss, e, T):column(boss, e, T) + 64] for e in d], "cq", T, topo)
     g.wait_ge(T.sem.loc, n)
 
 
@@ -112,7 +153,6 @@ def rank_program(g, core, T, topo):
     cls = 0 if core in two[0] else 1
     mine = pieces.index(core)
     idx = two[cls].index(core)
-    rk = [T.rank_of(c) for c in pieces]
 
     Q = {"v": [g.vector, "cv"], "s": [g.scalar, None], "t": [g.tensor, None], "g": [g, None], "y": [g.sync, None]}
     total = {}
@@ -152,41 +192,32 @@ def rank_program(g, core, T, topo):
     lx = run("s", g.scalar.dma_start(T.xb[:], T.x[:]), "lx", 16)
 
     iota(T.pi[:], [[0, 1]], 0, 1, "kio0")
-    kio0 = iota(T.c64[:], [[1, 4], [0, 16]], 0, 0, "kio0")
-    iota(T.d64[:], [[0, 16], [1, 4]], 0, 0)
-    iota(T.k8[:], [[64, 8]], -1, 0)
-    kio = iota(T.v0[:], [[4, 16], [64, 16]], 0, 0)
+    kio0 = iota(T.p4[:], [[0, 1]], 48, 4, "kio0")
+    iota(T.c64[:], [[1, 4], [0, 16]], 0, 0)
+    kio = iota(T.val[:], [[4, 16], [64, 16]], 0, 0)
 
     kzz = V("set", T.zz[:], 0.0, key="kzz")
+    wait("v", kio0)
+    V("ts", T.pj[:, 0:1], T.pi[:], 3, None, A.bitwise_and)
+    V("ts", T.pj[:, 1:2], T.pi[:], 15, None, A.bitwise_and)
+    t = V("ts", T.pj[:, 2:3], T.pi[:], 2, 28, A.arith_shift_right, A.bitwise_and)
     kz = V("set", T.zb[:], 0.0, key="kz")
+    tp = V("cp", T.pf[:, 0:1], T.pj[:, 0:1], deps=[t])
+    pt = T.pf[:, 0:1]
+    V("ts", T.uo[:, 2:3], T.pj[:, 1:2], -3.0, T.p4[:], A.mult, A.add)
     kxp = V("q", T.xq[:, 256:384], T.xp[:, 256:384], T.zz[:], deps=[kzz], key="kxp")
+    t = V("ts", T.uo[:, 0:1], T.pj[:, 2:3], pt, None, A.add, deps=[tp])
 
     def zero(block, key):
         return S(T.wz[:, 512 * block:512 * block + 512], T.zz[:], deps=[kzz], key=key)
-    zero(0, "kw0")
-    zero(1, "kw0")
-    zs = ksz = None
-    for l in range(4):
-        for e in range(4):
-            a = 4 * (12 + l) + e
-            o, i = T.zb[:, a:a + 449:64], T.usl[:, e:32:4]
-            if l < 2:
-                zs = V("cp", o, i, deps=[kz, lus])
-            else:
-                ksz = S(o, i, deps=[kz, lus], key="kzs")
-    kzq = V("q", T.zq[:], T.zp[:], T.zb[:], deps=[zs, ksz], key="kzq")
+    for h in range(7):
+        zero(h, "kw0" if h < 4 else "kw1")
+    t = V("cp", T.u16[:], T.usl[:, 0:32].indirect(T.uo[:, 0:1]), deps=[t, lus])
+    t = V("cp", T.zb[:, 0:560].indirect(T.uo[:, 2:3]), T.u16[:], deps=[t, kz])
+    kzq = V("q", T.zq[:], T.zp[:], T.zb[:], deps=[t], key="kzq")
     kxq = V("q", T.xq[:, 0:256], T.xp[:, 0:256], T.xb[:], deps=[lx], key="kxq")
-    zero(2, "kw0")
-    kw0 = zero(3, "kw0")
-    zero(4, "kw1")
-    zero(5, "kw1")
-    wait("v", kio0)
-    V("ts", T.pj[:, 0:1], T.pi[:], 3, None, A.bitwise_and)
-    V("ts", T.pj[:, 1:2], T.pi[:], 2, 3, A.arith_shift_right, A.bitwise_and)
-    t = V("ts", T.pj[:, 2:3], T.pi[:], 15, None, A.bitwise_and)
-    kpf = V("cp", T.pf[:, 0:3], T.pj[:, 0:3], deps=[t], key="kpf")
-    pt, pa, pqq = T.pf[:, 0:1], T.pf[:, 1:2], T.pf[:, 2:3]
-    tm = V("ts", T.msk[:], T.c64[:], pt, None, A.is_equal, deps=[kpf])
+    tm = V("ts", T.msk[:], T.c64[:], pt, None, A.is_equal, deps=[kio])
+    kw7 = V("set", T.wz[:, 512 * 7:512 * 8], 0.0, key="kw7")
 
     wait("t", kzq, kxp, kxq)
     for i in range(4):
@@ -206,41 +237,43 @@ def rank_program(g, core, T, topo):
     def arriving(c, *kinds):
         return sum(len(topo.engines(h, core)) for k in kinds for h, d in theirs[c][k].items() if core in d)
     nB = sum(arriving(c, "scores") for c in far)
-    kc = ("kc", sum(len(topo.engines(h, far[0])) for h in hs))
+    kc = ("kc", sum(len(topo.engines(h, near[0])) for h in road["helpers"]))
     wait("g", ksc)
-    loc = write(g, core, hs, eon, own, T.rsc[:], "rs0", T, topo)
-    loc += write(g, core, near, eoff, own, own, "scA", T, topo)
+    loc = write(g, core, hs, eon, own, [T.rsc[:]] * len(hs), "rs0", T, topo)
+    loc += write(g, core, near, eoff, own, [own] * len(near), "scA", T, topo)
 
-    ksr = None
-    for i in range(4):
-        ksr = S(T.repa[:, 16 * i:16 * i + 16], own, deps=[ksc], key="ksr")
-    kpz = S(T.pk[:, 256:512], T.zz[:, 0:256], deps=[kzz], key="kpz")
-    zero(6, "kw1")
-    kw1 = zero(7, "kw1")
-    t = V("set", T.rm[:], 1.0)
-    V("set", T.la[:, 16 * idx:16 * idx + 16], 0.0)
-    V("set", T.tb[:], 0.0)
-    V("set", T.ts[:], 0.0)
-    V("set", T.ts2[:, 0:1], 0.0)
-    V("set", T.inv[:, 0:64], 0.0)
-    V("set", T.rm[:, 0:128:16], 0.0, deps=[t])
-    kval = S(T.val[:], T.v0[:], deps=[kio, kpf], key="kval", bias=pt)
-    for i in range(8):
-        kpr = S(T.prio[:, 16 * i:16 * i + 16], T.one[:], deps=[kc], key="kpr", scale=float(8 - rk[i]))
-    for half, kw in enumerate((kw0, kw1)):
-        wait("y", kw)
+    for half, kw in enumerate(([("kw0", 4)], [("kw1", 3), kw7])):
+        wait("y", *kw)
         for h in range(4 * half, 4 * half + 4):
             run("y", g.sync.dma_start(T.wz[16 * h:16 * h + 16, 512 * h:512 * h + 512], T.w[16 * h:16 * h + 16, :]), "lw%d" % half, 16)
 
     def wquant(half):
         V("q", T.wq[:, 512 * half:512 * half + 512], T.wp[:, 512 * half:512 * half + 512],
           T.wz[:, 2048 * half:2048 * half + 2048], deps=[("lw%d" % half, 64)], key="kwq%d" % half)
-    wait("v", kio)
-    V("ts", T.m4[:], T.d64[:], 1.0, None, A.min)
-    V("ts", T.mk2[:], T.d64[:], pa, None, A.is_equal)
-    t = V("ts", T.qr[:], pqq, float(ROW), float(ROW + 1), A.mult, A.add)
+
+    ksr = None
+    for i in range(4):
+        ksr = S(T.repa[:, 16 * i:16 * i + 16], own, deps=[ksc], key="ksr")
+    kpz = S(T.pk[:, 256:512], T.zz[:, 0:256], deps=[kzz], key="kpz")
+    t = V("set", T.rm[:], 1.0)
+    V("set", T.la[:, 16 * idx:16 * idx + 16], 0.0)
+    V("set", T.tb[:], 0.0)
+    V("set", T.ts[:], 0.0)
+    V("set", T.ts2[:, 0:1], 0.0)
+    V("set", T.inv[:, 0:64], 1020.0)
+    V("set", T.rm[:, 0:128:16], 0.0, deps=[t])
     wquant(0)
-    V("ts", T.pc[:], T.pc0[:], T.qr[:], None, A.add, deps=[t, kc])
+    wquant(1)
+
+    def seated(ranks, dep):
+        k = None
+        for c in ranks:
+            a, b = 16 * [seat(k) for k in range(N)].index(T.rank_of(c)), 16 * pieces.index(c)
+            k = S(T.st[:, a:a + 16], T.sc[:, b:b + 16], deps=[dep], key="kst")
+        return k
+    seated([core], ksc)
+    seated(near, ("scA", nA))
+    kst = seated(far, ("scB", nB))
 
     ca, cb = 64 * cls, 64 * (1 - cls)
     wait("v", ksr, ("scA", nA), ksc)
@@ -254,9 +287,8 @@ def rank_program(g, core, T, topo):
     t = V("ts", T.pen[:], T.la3[:], -1e28, None, A.mult, deps=[t])
     for i in range(4):
         tr = V("tt", T.repb[:, 16 * i:16 * i + 16], own, T.pen[:], A.add, deps=[t] if i == 0 else [])
-    wquant(1)
 
-    wait("v", tr, ("scB", nB))
+    wait("v", tr, kc, ("scB", nB))
     low = 16 * len([c for c in far if T.rank_of(c) < rank])
     if low > 0:
         t = V("tt", T.cb[:, 0:low], T.sc[:, cb:cb + low], T.repb[:, 0:low], A.is_ge)
@@ -264,53 +296,55 @@ def rank_program(g, core, T, topo):
         t = V("tt", T.cb[:, low:64], T.sc[:, cb + low:cb + 64], T.repb[:, low:64], A.is_gt)
     t = V("tt", T.cb2[:], T.cb[:, 0:32], T.cb[:, 32:64], A.max, deps=[t])
     t = V("tt", T.lose[:], T.cb2[:, 0:16], T.cb2[:, 16:32], A.max, deps=[t])
-    t = V("scan", T.tb[:, 0:16], T.one[:], T.lose[:], -1.0, A.add, A.subtract, deps=[t, kc])
+    t = V("scan", T.tb[:, 0:16], T.one[:], T.lose[:], 0.0, A.add, A.subtract, deps=[t])
     tw = V("tt", T.lp[:], T.lose[:], T.pc[:], A.mult, key="cw")
     t = V("tr", T.tt[:], T.tb[:], deps=[t])
     tw = V("tt", T.fo[:], T.tb[:, 0:16], T.lp[:], A.add, deps=[tw], key="cw")
     t = V("scan", T.ts[:, 1:32], T.tt[:, 0:31], T.rm[:, 1:32], 0.0, A.add, A.mult, deps=[t])
     t = V("tr", T.bt[:], T.ts[:], deps=[t])
-    t = V("ts", T.offa[:], T.fo[:], T.bt[:, 15:16], pqq, A.add, A.add, deps=[t, tw, kpf])
-    t = V("cp", T.inv[:, 0:WIN].indirect(T.offa[:, 0:16]), T.val[:], deps=[t, kval])
-    t = V("tt", T.mkd[:], T.inv[:, 0:64], T.mk2[:], A.mult, deps=[t])
-    t = V("scan", T.sel[:], T.m4[:], T.mkd[:], 0.0, A.mult, A.add, deps=[t])
-    t = V("cp", T.offb[:], T.sel[:, 3:64:4], deps=[t])
-    t = V("cp", T.pk[:, 0:256], T.xb[:, 0:1024].indirect(T.offb[:, 0:16]), deps=[t])
-    kpk = V("q", T.oq[:], T.op[:], T.pk[:], deps=[t, kpz], key="kpk")
+    t = V("ts", T.offa[:], T.fo[:], T.bt[:, 15:16], -1.0, A.add, A.add, deps=[t, tw])
+    t = V("cp", T.inv[:, 0:WIN].indirect(T.offa[:, 0:16]), T.val[:], deps=[t])
+    t = V("scan", T.sel[:], T.a4[:], T.inv[:, 0:64], 0.0, A.add, A.min, deps=[t])
+    kob = V("ts", T.offb[:], T.sel[:, 3:64:4], pt, None, A.add, deps=[t], key="kob")
+    kg = S(T.pk[:, 128:256], T.xb[:, 0:1024].indirect(T.offb[:, 8:16]), deps=[kob], key="kg")
+    t = V("cp", T.pk[:, 0:128], T.xb[:, 0:1024].indirect(T.offb[:, 0:8]), deps=[kob])
+    kpk = V("q", T.pq[:, OWN:OWN + 128], T.pp[:, OWN:OWN + 128], T.pk[:], deps=[t, kg, kpz], key="kpk")
 
-    c0 = 64 * mine
-    oq, pq = T.oq[:, 0:64].bitcast(dt.uint8), T.pq[:, c0:c0 + 64].bitcast(dt.uint8)
-    op, pp = T.op[:, 0:64], T.pp[:, c0:c0 + 64]
+    oq, op = T.pq[:, OWN:OWN + 64].bitcast(dt.uint8), T.pp[:, OWN:OWN + 64]
     wait("g", kpk)
-    loc += write(g, core, list(road["codes"]), every, oq, T.rq[:].bitcast(dt.uint8), "rs1", T, topo)
-    loc += write(g, core, road["handed"], every, op, T.rp[:], "rs2", T, topo)
-    loc += write(g, core, near, eoff, oq, pq, "cqA", T, topo)
-    wait("y", kpk)
-    run("y", g.sync.dma_start(pq, oq), "lown", 16)
-    run("y", g.sync.dma_start(pp, op), "lown", 16)
+    loc += write(g, core, list(road["codes"]), every, oq, [T.rq[:].bitcast(dt.uint8)] * len(road["codes"]), "rs1", T, topo)
+    loc += write(g, core, list(road["planes"]), every, op, [T.rp[:]] * len(road["planes"]), "rs2", T, topo)
+    loc += write(g, core, near, eoff, oq, [T.pq[:, column(core, c, T):column(core, c, T) + 64].bitcast(dt.uint8) for c in near],
+                 "cq", T, topo)
 
-    t = V("tt", T.m64[:], T.sc[:, 0:64], T.sc[:, 64:128], A.max)
-    t = V("tt", T.m32[:], T.m64[:, 0:32], T.m64[:, 32:64], A.max, deps=[t])
-    for i in range(2):
-        tm = V("tt", T.m16[:, 16 * i:16 * i + 16], T.m32[:, 0:16], T.m32[:, 16:32], A.max, deps=[t] if i == 0 else [])
-    for i in range(4):
-        t = V("tt", T.eq[:, 32 * i:32 * i + 32], T.sc[:, 32 * i:32 * i + 32], T.m16[:], A.is_equal, deps=[tm] if i == 0 else [])
-    t = V("tt", T.eqp[:], T.eq[:], T.prio[:], A.mult, deps=[t, kpr])
-    t = V("tt", T.e64[:], T.eqp[:, 0:64], T.eqp[:, 64:128], A.max, deps=[t])
-    t = V("tt", T.e32[:], T.e64[:, 0:32], T.e64[:, 32:64], A.max, deps=[t])
-    for i in range(2):
-        tm = V("tt", T.pv[:, 16 * i:16 * i + 16], T.e32[:, 0:16], T.e32[:, 16:32], A.max, deps=[t] if i == 0 else [])
-    for i in range(4):
-        kwin = V("tt", T.win[:, 32 * i:32 * i + 32], T.pv[:], T.prio[:, 32 * i:32 * i + 32], A.is_equal,
-                 deps=[tm] if i == 0 else [], key="kwin")
+    def product(h, a, b, bank, key, deps):
+        wait("t", *deps)
+        return run("t", g.tensor.matmul_mx(T.ps[:, 512 * bank:512 * bank + b - a], T.wq[:, 128 * h:128 * h + 128],
+                                           T.wp[:, 128 * h:128 * h + 128], T.pq[:, a:b], T.pp[:, a:b], True, True), key)
+
+    def drain(h, a, b, bank, key, k):
+        return S(T.res[:, 512 * h + a:512 * h + b], T.ps[:, 512 * bank:512 * bank + b - a], deps=[k], key=key)
+    wait("t", ("kwq0", 1), ("kwq1", 1), kpsr, kpk)
+    ma = [product(h, OWN, OWN + 128, h, "ma%d" % h, []) for h in range(8)]
+
+    t = V("tt", T.m1[:], T.st[:, 0:64], T.st[:, 64:128], A.max, deps=[kst])
+    V("tt", T.g1[:], T.st[:, 64:128], T.st[:, 0:64], A.is_gt, key="cw")
+    t = V("tt", T.m2[:], T.m1[:, 0:32], T.m1[:, 32:64], A.max, deps=[t])
+    tw = V("tt", T.g2[:], T.m1[:, 32:64], T.m1[:, 0:32], A.is_gt, key="cw")
+    V("tt", T.w3[:, 16:32], T.m2[:, 16:32], T.m2[:, 0:16], A.is_gt, deps=[t])
+    t = V("tt", T.w3[:, 0:16], T.m2[:, 0:16], T.m2[:, 16:32], A.is_ge)
+    t = V("tt", T.w2[:, 32:64], T.w3[:], T.g2[:], A.mult, deps=[t, tw])
+    t = V("tt", T.w2[:, 0:32], T.w3[:], T.w2[:, 32:64], A.subtract, deps=[t])
+    t = V("tt", T.win[:, 64:128], T.w2[:], T.g1[:], A.mult, deps=[t])
+    kwin = V("tt", T.win[:, 0:64], T.w2[:], T.win[:, 64:128], A.subtract, deps=[t], key="kwin")
+    da = [drain(h, OWN, OWN + 64, h, "da%d" % h, ma[h]) for h in range(8)]
     kw2 = S(T.win2[:], T.win[:], deps=[kwin], key="kw2")
-    kwn = S(T.wnv[:], T.pv[:, 0:16], deps=[kwin], key="kwn", scale=-1.0, bias=8.0)
     t = V("scan", T.cum[:], T.rm[:], T.win[:], 0.0, A.mult, A.add, deps=[kwin])
     t = V("tr", T.t2[:], T.cum[:], deps=[t])
     t = V("scan", T.ts2[:, 1:128], T.t2[:, 0:127], T.rm[:, 1:128], 0.0, A.add, A.mult, deps=[t])
+    tw = V("tt", T.win2[:, 0:128:16], T.win2[:, 0:128:16], T.k8[:], A.add, deps=[kw2], key="cw")
     t = V("tr", T.b2[:], T.ts2[:], deps=[t])
-    t = V("tt", T.bk[:], T.b2[:, 15:128:16], T.k8[:], A.add, deps=[t])
-    t = V("tt", T.win2[:, 0:128:16], T.win2[:, 0:128:16], T.bk[:], A.add, deps=[t, kw2])
+    t = V("tt", T.win2[:, 0:128:16], T.win2[:, 0:128:16], T.b2[:, 15:128:16], A.add, deps=[t, tw])
     t = V("scan", T.cu2[:], T.rm[:], T.win2[:], 0.0, A.mult, A.add, deps=[t])
     t = V("tt", T.pr[:], T.cu2[:], T.win[:], A.mult, deps=[t])
     t = V("tt", T.f64[:], T.pr[:, 0:64], T.pr[:, 64:128], A.add, deps=[t])
@@ -319,41 +353,33 @@ def rank_program(g, core, T, topo):
     t = V("tt", T.x1[:, 16:32], T.f32[:, 0:16], T.f32[:, 16:32], A.add)
     V("tr", T.t1[0:64, 0:32], T.x1[0:64, :], deps=[t])
     t = V("tr", T.t1[64:128, 32:64], T.x1[64:128, :])
+    tw = V("cp", T.wi[:], T.x1[:, 0:16], key="cw")
     V("cp", T.t1[64:128, 0:32], T.t1[0:64, 0:32], deps=[t])
     t = V("cp", T.t1[0:64, 32:64], T.t1[64:128, 32:64])
+    kfr = V("tt", T.fr[:], T.x1[:, 0:16], T.wi[:], A.subtract, deps=[tw], key="kfr")
     for e in range(2):
         for b in range(4):
             a = b // 2 * 2 + e
             t = V("cp", T.off[32 * b:32 * b + 32, 64 * e:64 * e + 64], T.t1[32 * a:32 * a + 32, 0:64], deps=[t] if e + b == 0 else [])
     toff = t
-    wait("y", kwn)
+    kwn = S(T.wnv[:], T.fr[:], deps=[kfr], key="kwn", scale=16.0)
+    wait("g", ("loc", loc))
+    wait("y", kwn, ("loc", loc))
     run("y", g.sync.dma_start(T.wn[:], T.wnv[:]), "lwn", 16)
 
-    def product(h, half, bank, key, deps):
-        wait("t", *deps)
-        return run("t", g.tensor.matmul_mx(T.ps[:, 512 * bank:512 * bank + 256], T.wq[:, 128 * h:128 * h + 128], T.wp[:, 128 * h:128 * h + 128],
-                                           T.pq[:, 256 * half:256 * half + 256], T.pp[:, 256 * half:256 * half + 256], True, True), key)
-
-    def drain(h, half, bank, key, k):
-        o = 512 * h + 256 * half
-        return S(T.res[:, o:o + 256], T.ps[:, 512 * bank:512 * bank + 256], deps=[k], key=key)
-    da, db = {}, {}
-    wait("t", ("kwq0", 1), ("kwq1", 1), kpsr, ("cqB", sum(arriving(c, "codes", "planes") for c in far)))
-    mb = [product(h, 1 - cls, h, "mb%d" % h, []) for h in range(8)]
-    for h in range(FIRST):
-        db[h] = drain(h, 1 - cls, h, "db%d" % h, mb[h])
-    wait("t", ("lown", 32), ("cqA", sum(len(eoff) + arriving(c, "nplanes") for c in near)))
-    for h in range(8):
-        bank = h % FIRST
-        if h >= FIRST:
-            db[h] = drain(h, 1 - cls, h, "db%d" % h, mb[h])
-        da[h] = drain(h, cls, bank, "da%d" % h, product(h, cls, bank, "ma%d" % h, [db[h] if h < FIRST else da[h - FIRST]]))
+    wait("t", ("cq", sum(len(eoff) + arriving(c, "planes") for c in near) + sum(arriving(c, "codes", "planes") for c in far)))
+    mb = [product(0, 0, OWN // 2, 0, "mb0", [da[0]])]
+    md = product(0, OWN // 2, OWN, 7, "md", [da[7]])
+    mb += [product(h, 0, OWN, h, "mb%d" % h, [da[h]]) for h in range(1, 7)]
+    dd = V("cp", T.res[:, OWN // 2:OWN], T.ps[:, 512 * 7:512 * 7 + OWN // 2], deps=[md], key="dd")
+    mb.append(product(7, 0, OWN, 7, "mb7", [dd]))
+    db = [drain(h, 0, OWN // (2 if h == 0 else 1), h, "db%d" % h, mb[h]) for h in range(8)]
 
     def found(h, a, b):
         o = 64 * (h // 2 % 2) + 32 * (h // 4) + 16 * (h % 2)
         return T.res[:, 512 * h:512 * h + 512].indirect(T.off[:, o + a // 16:o + b // 16])
     out, prev = T.ya, T.yb
-    acc = V("cp", out[:], found(0, 0, 256), deps=[toff, da[0], db[0]])
+    acc = V("cp", out[:], found(0, 0, 256), deps=[toff, da[0], db[0], dd])
     for h in range(1, 7):
         out, prev = prev, out
         acc = V("tt", out[:], found(h, 0, 256), prev[:], A.add, deps=[acc, da[h], db[h]])
@@ -364,5 +390,6 @@ def rank_program(g, core, T, topo):
         wait(q, k)
         run(q, Q[q][0].dma_start(T.y[:, a:b], out[:, a:b]), "ly", 16)
 
-    wait("g", ("ly", 32), ("lwn", 16), ("loc", loc))
+    wait("g", ("ly", 32), ("lwn", 16))
     g.wait_ge(T.sem.cv, total["cv"])
+    g.wait_ge(T.sem.cw, total["cw"])

@@ -379,16 +379,18 @@ def rank_program(g, core, T, topo):
         o = 64 * (h // 2 % 2) + 32 * (h // 4) + 16 * (h % 2)
         return T.res[:, 512 * h:512 * h + 512].indirect(T.off[:, o + a // 16:o + b // 16])
     out, prev = T.ya, T.yb
-    acc = V("cp", out[:], found(0, 0, 256), deps=[toff, da[0], db[0], dd])
-    for h in range(1, 7):
+    acc = [None, None]
+    for h in range(8):
         out, prev = prev, out
-        acc = V("tt", out[:], found(h, 0, 256), prev[:], A.add, deps=[acc, da[h], db[h]])
-    out, prev = prev, out
+        for i in range(2):
+            a, b = 128 * i, 128 * i + 128
+            if h == 0:
+                acc[i] = V("cp", out[:, a:b], found(0, a, b), deps=[toff, da[0], db[0], dd], key="ky%d" % i)
+            else:
+                acc[i] = V("tt", out[:, a:b], found(h, a, b), prev[:, a:b], A.add, deps=[acc[i], da[h], db[h]], key="ky%d" % i)
     for i, q in enumerate(("y", "s")):
-        a, b = 128 * i, 128 * i + 128
-        k = V("tt", out[:, a:b], found(7, a, b), prev[:, a:b], A.add, deps=[acc, da[7], db[7]], key="ky%d" % i)
-        wait(q, k)
-        run(q, Q[q][0].dma_start(T.y[:, a:b], out[:, a:b]), "ly", 16)
+        wait(q, acc[i])
+        run(q, Q[q][0].dma_start(T.y[:, 128 * i:128 * i + 128], out[:, 128 * i:128 * i + 128]), "ly", 16)
 
     wait("g", ("ly", 32), ("lwn", 16))
     g.wait_ge(T.sem.cv, total["cv"])

@@ -4,8 +4,9 @@ from concourse.mybir import dt, AluOpType as A, ActivationFunctionType
 N = 8
 CODES = "float8_e4m3fn_x4"
 ROW = 80
-WIN = 129 * ROW
+WIN = 130 * ROW
 OWN = 64 * (N - 1)
+BIG = 1.5 * 2.0 ** 26
 
 
 def sb(kind, **cols):
@@ -17,19 +18,21 @@ SCRATCH.update(sb("bfloat16", xb=1024, usl=32, u16=16, zb=560, pk=512, wz=4096, 
 SCRATCH.update(sb(CODES, zq=140, xq=384, wq=1024, pq=576, rq=64))
 SCRATCH.update(sb("uint8", zp=140, xp=384, wp=1024, pp=576, rp=64))
 SCRATCH.update(sb("int32", pi=1, pj=4, wi=16))
-SCRATCH.update(sb("float32", pf=4, p4=1, c64=64, d64=64, msk=64, val=256, pc=16, one=16, k8=8))
-SCRATCH.update(sb("bfloat16", rm=128, a4=64))
-SCRATCH.update(sb("float32", rsc=16, sm=64, s32=32, sc=128, repa=64, repb=64, la=64, la2=32, la3=16, pen=16, cb=64, cb2=32,
-                  lose=16, tb=32, tt=32, ts=32, bt=32, lp=16, fo=16, inv=WIN, sel=64))
+SCRATCH.update(sb("float32", pf=4, p4=1, c64=64, d64=32, msk=64, val=256, pc=16, k8=8))
+SCRATCH.update(sb("bfloat16", rm=128, a4=64, z8=128))
+SCRATCH.update(sb("float32", rsc=16, sm=64, s32=32, sc=128, lose=16, lp=16, fo=16, inv=WIN, sel=64))
+SCRATCH.update(sb("bfloat16", fl=128, cs=136, tt=32, ts=32, bt=32))
 SCRATCH.update(sb("uint16", uo=4, offa=16, offb=16, off=128))
 SCRATCH.update(sb("bfloat16", win=128, cum=128, t2=128, ts2=128, b2=128))
-SCRATCH.update(sb("float32", st=128, g1=64, m1=64, g2=32, m2=32, w3=32, w2=64, win2=128, cu2=128, pr=128, f64=64, f32=32,
-                  x1=32, t1=64, fr=16, wnv=16, res=4096, ya=256, yb=256))
-SEMAPHORES = (["cv", "cw", "loc", "scA", "scB", "cq", "rs0", "rs1", "rs2", "kc",
-               "lus", "lx", "lw0", "lw1", "lwn", "ly",
-               "kz", "kzz", "kzq", "kxp", "kxq", "ksc", "ksr", "kps", "kpsr", "kio", "kio0", "kpz", "kst", "kob", "kg",
-               "kw0", "kw1", "kw7", "kwq0", "kwq1", "kfr", "md", "dd",
-               "kpk", "kwn", "kwin", "kw2", "ky0", "ky1"] + ["%s%d" % (k, h) for k in ("ma", "da", "mb", "db") for h in range(8)])
+SCRATCH.update(sb("float32", st=128, g1=64, n1=64, m1=64, g2=32, n2=32, m2=32, w3=32, w2=64, win2=128, cu2=128, pr=128, f64=64,
+                  f32=32, x1=32, t1=64, fr=16, wnv=16, res=4096, ya=256, yb=256))
+CHAINS = ["cv", "cw", "cx", "cy"]
+SEMAPHORES = (CHAINS + ["loc", "cq", "rs0", "rs1", "rs2", "kc",
+                        "lus", "lx", "lw0", "lw1", "lwn", "ly",
+                        "kz", "kzz", "kzq", "kxp", "kxq", "ksc", "kps", "kpsr", "kio", "kio0", "kpz", "kst", "kob", "kg",
+                        "kw0", "kw1", "kw7", "kwq0", "kwq1", "kg1", "kn1", "md", "dd",
+                        "kpk", "kwn", "kwin", "kw2", "ky0", "ky1"]
+              + ["%s%d" % (k, h) for k in ("ma", "da", "mb", "db", "sc") for h in range(8)])
 
 
 def order(T, topo):
@@ -40,17 +43,16 @@ def order(T, topo):
 def roads(core, T, topo):
     two = order(T, topo)
     own, far = two if core in two[0] else two[::-1]
-    near = [c for c in own if c != core]
+    k = own.index(core)
+    near = own[k + 1:] + own[:k]
+    far = far[k:] + far[:k]
     free = [c for c in topo.cores_of(core) if c not in T.cores]
     cand = [c for c in free if all(topo.may_write(c, d) for d in far)]
     a = [c for c in cand if topo.die(c) != topo.die(core)]
     b = [c for c in cand if topo.die(c) == topo.die(core)]
     rest = [c for c in free if c not in cand and topo.die(c) != topo.die(core)]
-    hc, hp = [a[0], b[0]], [a[1], b[1]]
-    k = own.index(core)
-    codes = {h: [d for j, d in enumerate(far) if (j + k) % 2 == i] for i, h in enumerate(hc)}
-    planes = {h: [d for j, d in enumerate(far) if (j + k) % 2 == i] for i, h in enumerate(hp)}
-    planes.update({rest[0]: near[:2], rest[1]: near[2:]})
+    codes = {a[0]: far[0::2], b[0]: far[1::2]}
+    planes = {a[1]: far[0::2], b[1]: far[1::2], rest[0]: near[:2], rest[1]: near[2:]}
     return {"near": near, "far": far, "codes": codes, "planes": planes, "scores": codes, "helpers": list(codes) + list(planes)}
 
 
@@ -87,30 +89,25 @@ def whole(g, out, pattern, base, cm, sem):
 
 def constant(g, which, boss, T):
     v, kio, cv = g.vector, T.sem.kio, T.sem.cv
-    if which < 2:
-        out = T.one[:, 8 * which:8 * which + 8]
-        whole(g, out, [[0, 8]], 1, 0, kio)
-    elif which < 4:
-        a = 8 * (which - 2)
-        out = T.pc[:, a:a + 8]
-        whole(g, out, [[1, 8]], ROW + 1 + a, ROW, kio)
-    elif which == 4:
-        out = T.k8[:]
-        for k in range(N):
-            v.memset(T.k8[:, k:k + 1], column(T.cores[seat(k)], boss, T) - 1 + seat(k) / 16).then_inc(kio, 1)
-        g.wait_ge(kio, N)
-        return out
-    else:
-        out = T.a4[:]
+    half, n = which % 2, 1
+    if which // 2 == 0:
+        out = T.pc[:, 8 * half:8 * half + 8]
+        whole(g, out, [[N, 8]], N * (ROW + 1 + 8 * half), N * ROW, kio)
+    elif which // 2 == 1:
+        out = T.a4[:, 32 * half:32 * half + 32]
         whole(g, T.pi[:], [[0, 1]], 0, 1, cv)
-        whole(g, T.d64[:], [[0, 16], [1, 4]], 0, 0, cv)
+        whole(g, T.d64[:], [[0, 8], [1, 4]], 0, 0, cv)
         v.wait_ge(cv, 2)
         v.tensor_scalar(T.pj[:, 0:1], T.pi[:], 2, 3, A.arith_shift_right, A.bitwise_and).then_inc(cv, 1)
         v.wait_ge(cv, 3)
         v.tensor_copy(T.pf[:, 0:1], T.pj[:, 0:1]).then_inc(cv, 1)
         v.wait_ge(cv, 4)
         v.tensor_scalar(out, T.d64[:], T.pf[:, 0:1], 2048.0, A.is_equal, A.mult).then_inc(kio, 1)
-    g.wait_ge(kio, 1)
+    else:
+        out, n = T.k8[:, 4 * half:4 * half + 4], 4
+        for k in range(4 * half, 4 * half + 4):
+            v.memset(T.k8[:, k:k + 1], column(T.cores[seat(k)], boss, T) - 1 + seat(k) / 16).then_inc(kio, 1)
+    g.wait_ge(kio, n)
     return out
 
 
@@ -126,7 +123,7 @@ def relay(g, core, boss, T, topo):
     if core in r["scores"]:
         g.wait_ge(T.sem.rs0, len(eon))
         d = r["scores"][core]
-        n += write(g, core, d, eng, T.rsc[:], [T.sc[:, 16 * p:16 * p + 16]] * len(d), "scB", T, topo)
+        n += write(g, core, d, eng, T.rsc[:], [T.sc[:, 16 * p:16 * p + 16]] * len(d), "sc%d" % p, T, topo)
     if core in r["codes"]:
         g.wait_ge(T.sem.rs1, len(every))
         d = r["codes"][core]
@@ -148,11 +145,8 @@ def rank_program(g, core, T, topo):
         return
     road = roads(core, T, topo)
     near, far = road["near"], road["far"]
-    two = order(T, topo)
-    pieces = two[0] + two[1]
-    cls = 0 if core in two[0] else 1
+    pieces = sum(order(T, topo), [])
     mine = pieces.index(core)
-    idx = two[cls].index(core)
 
     Q = {"v": [g.vector, "cv"], "s": [g.scalar, None], "t": [g.tensor, None], "g": [g, None], "y": [g.sync, None]}
     total = {}
@@ -163,7 +157,7 @@ def rank_program(g, core, T, topo):
             if d is None:
                 continue
             sem, val = d
-            if sem in ("cv", "cw"):
+            if sem in CHAINS:
                 val = total[sem]
             if seen[q].get(sem, 0) < val:
                 Q[q][0].wait_ge(T.sem[sem], val)
@@ -197,15 +191,15 @@ def rank_program(g, core, T, topo):
     kio = iota(T.val[:], [[4, 16], [64, 16]], 0, 0)
 
     kzz = V("set", T.zz[:], 0.0, key="kzz")
+    kz = V("set", T.zb[:], 0.0, key="kz")
     wait("v", kio0)
     V("ts", T.pj[:, 0:1], T.pi[:], 3, None, A.bitwise_and)
     V("ts", T.pj[:, 1:2], T.pi[:], 15, None, A.bitwise_and)
     t = V("ts", T.pj[:, 2:3], T.pi[:], 2, 28, A.arith_shift_right, A.bitwise_and)
-    kz = V("set", T.zb[:], 0.0, key="kz")
+    kxp = V("q", T.xq[:, 256:384], T.xp[:, 256:384], T.zz[:], deps=[kzz], key="kxp")
     tp = V("cp", T.pf[:, 0:1], T.pj[:, 0:1], deps=[t])
     pt = T.pf[:, 0:1]
     V("ts", T.uo[:, 2:3], T.pj[:, 1:2], -3.0, T.p4[:], A.mult, A.add)
-    kxp = V("q", T.xq[:, 256:384], T.xp[:, 256:384], T.zz[:], deps=[kzz], key="kxp")
     t = V("ts", T.uo[:, 0:1], T.pj[:, 2:3], pt, None, A.add, deps=[tp])
 
     def zero(block, key):
@@ -225,22 +219,26 @@ def rank_program(g, core, T, topo):
                                T.xq[:, 64 * i:64 * i + 128], T.xp[:, 64 * i:64 * i + 128], i == 0, i == 3)
     kps = run("t", m, "kps")
     kpsr = V("tt", T.sm[:], T.ps[:, 0:64], T.msk[:], A.mult, deps=[kps, tm], key="kpsr")
+    V("set", T.rm[:], 1.0, key="cw")
+    V("set", T.z8[:], 0.0, key="cw")
     t = V("tt", T.s32[:], T.sm[:, 0:32], T.sm[:, 32:64], A.add, deps=[kpsr])
+    V("set", T.ts[:, 0:1], 0.0, key="cw")
+    tw = V("set", T.ts2[:, 0:1], 0.0, key="cw")
     own = T.sc[:, 16 * mine:16 * mine + 16]
     ksc = V("tt", own, T.s32[:, 0:16], T.s32[:, 16:32], A.add, deps=[t], key="ksc")
 
     hs = list(road["scores"])
     eoff, eon, every = engines_of(core, near[0], hs[0], topo)
-    nA = len(near) * len(eoff)
     theirs = {c: roads(c, T, topo) for c in near + far}
 
     def arriving(c, *kinds):
         return sum(len(topo.engines(h, core)) for k in kinds for h, d in theirs[c][k].items() if core in d)
-    nB = sum(arriving(c, "scores") for c in far)
+    landed = {c: ("sc%d" % pieces.index(c), len(eoff) if c in near else arriving(c, "scores")) for c in near + far}
+    others = sorted(near, key=lambda c: theirs[c]["near"].index(core)) + sorted(far, key=lambda c: theirs[c]["far"].index(core))
     kc = ("kc", sum(len(topo.engines(h, near[0])) for h in road["helpers"]))
     wait("g", ksc)
     loc = write(g, core, hs, eon, own, [T.rsc[:]] * len(hs), "rs0", T, topo)
-    loc += write(g, core, near, eoff, own, [own] * len(near), "scA", T, topo)
+    loc += write(g, core, near, eoff, own, [own] * len(near), "sc%d" % mine, T, topo)
 
     for half, kw in enumerate(([("kw0", 4)], [("kw1", 3), kw7])):
         wait("y", *kw)
@@ -251,63 +249,59 @@ def rank_program(g, core, T, topo):
         V("q", T.wq[:, 512 * half:512 * half + 512], T.wp[:, 512 * half:512 * half + 512],
           T.wz[:, 2048 * half:2048 * half + 2048], deps=[("lw%d" % half, 64)], key="kwq%d" % half)
 
-    ksr = None
-    for i in range(4):
-        ksr = S(T.repa[:, 16 * i:16 * i + 16], own, deps=[ksc], key="ksr")
     kpz = S(T.pk[:, 256:512], T.zz[:, 0:256], deps=[kzz], key="kpz")
-    t = V("set", T.rm[:], 1.0)
-    V("set", T.la[:, 16 * idx:16 * idx + 16], 0.0)
-    V("set", T.tb[:], 0.0)
-    V("set", T.ts[:], 0.0)
-    V("set", T.ts2[:, 0:1], 0.0)
-    V("set", T.inv[:, 0:64], 1020.0)
-    V("set", T.rm[:, 0:128:16], 0.0, deps=[t])
+    V("set", T.inv[:, 0:ROW], 1020.0)
+    V("set", T.cs[:, 0:N], 0.0)
+    V("set", T.fl[:, N - 1:128:N], BIG)
+    V("set", T.rm[:, 0:128:16], 0.0, deps=[tw])
+    V("set", T.z8[:, 0:128:N], N / 2 + 0.5)
+    V("set", T.z8[:, N - 1:128:N], BIG)
     wquant(0)
     wquant(1)
 
-    def seated(ranks, dep):
-        k = None
-        for c in ranks:
-            a, b = 16 * [seat(k) for k in range(N)].index(T.rank_of(c)), 16 * pieces.index(c)
-            k = S(T.st[:, a:a + 16], T.sc[:, b:b + 16], deps=[dep], key="kst")
-        return k
-    seated([core], ksc)
-    seated(near, ("scA", nA))
-    kst = seated(far, ("scB", nB))
+    def piece(c):
+        return T.sc[:, 16 * pieces.index(c):16 * pieces.index(c) + 16]
 
-    ca, cb = 64 * cls, 64 * (1 - cls)
-    wait("v", ksr, ("scA", nA), ksc)
-    a = 16 * idx
-    if idx > 0:
-        t = V("tt", T.la[:, 0:a], T.sc[:, ca:ca + a], T.repa[:, 0:a], A.is_ge)
-    if idx < 3:
-        t = V("tt", T.la[:, a + 16:64], T.sc[:, ca + a + 16:ca + 64], T.repa[:, a + 16:64], A.is_gt)
-    t = V("tt", T.la2[:], T.la[:, 0:32], T.la[:, 32:64], A.max, deps=[t])
-    t = V("tt", T.la3[:], T.la2[:, 0:16], T.la2[:, 16:32], A.max, deps=[t])
-    t = V("ts", T.pen[:], T.la3[:], -1e28, None, A.mult, deps=[t])
-    for i in range(4):
-        tr = V("tt", T.repb[:, 16 * i:16 * i + 16], own, T.pen[:], A.add, deps=[t] if i == 0 else [])
+    def seated(c, dep):
+        a = 16 * [seat(k) for k in range(N)].index(T.rank_of(c))
+        return S(T.st[:, a:a + 16], piece(c), deps=[dep], key="kst")
 
-    wait("v", tr, kc, ("scB", nB))
-    low = 16 * len([c for c in far if T.rank_of(c) < rank])
-    if low > 0:
-        t = V("tt", T.cb[:, 0:low], T.sc[:, cb:cb + low], T.repb[:, 0:low], A.is_ge)
-    if low < 64:
-        t = V("tt", T.cb[:, low:64], T.sc[:, cb + low:cb + 64], T.repb[:, low:64], A.is_gt)
-    t = V("tt", T.cb2[:], T.cb[:, 0:32], T.cb[:, 32:64], A.max, deps=[t])
-    t = V("tt", T.lose[:], T.cb2[:, 0:16], T.cb2[:, 16:32], A.max, deps=[t])
-    t = V("scan", T.tb[:, 0:16], T.one[:], T.lose[:], 0.0, A.add, A.subtract, deps=[t])
-    tw = V("tt", T.lp[:], T.lose[:], T.pc[:], A.mult, key="cw")
-    t = V("tr", T.tt[:], T.tb[:], deps=[t])
-    tw = V("tt", T.fo[:], T.tb[:, 0:16], T.lp[:], A.add, deps=[tw], key="cw")
+    def beaten(k, c, dep):
+        return V("tt", T.fl[:, k:128:N], piece(c), own, A.is_ge if T.rank_of(c) < rank else A.is_gt, deps=[dep])
+    seated(core, ksc)
+    wait("v", ksc, kc)
+    for k, c in enumerate(others):
+        kst = seated(c, landed[c])
+        t = beaten(k, c, landed[c])
+
+    t = V("scan", T.cs[:, N:], T.z8[:], T.fl[:], 0.0, A.add, A.subtract, deps=[t])
+    count = T.cs[:, 2 * N - 1::N]
+    t = V("tr", T.tt[:], T.cs[:, 104:136], deps=[t])
+    tw = V("tt", T.lose[:], count, T.cs[:, N - 1:128 + N - 1:N], A.is_equal, key="cw")
+    tx = V("tt", T.m1[:], T.st[:, 0:64], T.st[:, 64:128], A.max, deps=[kst], key="cx")
     t = V("scan", T.ts[:, 1:32], T.tt[:, 0:31], T.rm[:, 1:32], 0.0, A.add, A.mult, deps=[t])
+    tw = V("tt", T.lp[:], T.lose[:], T.pc[:], A.mult, deps=[tw], key="cw")
+    kg1 = V("tt", T.g1[:], T.st[:, 64:128], T.st[:, 0:64], A.is_gt, key="kg1")
+    kn1 = S(T.n1[:], T.g1[:], deps=[kg1], key="kn1", scale=-1.0, bias=1.0)
     t = V("tr", T.bt[:], T.ts[:], deps=[t])
-    t = V("ts", T.offa[:], T.fo[:], T.bt[:, 15:16], -1.0, A.add, A.add, deps=[t, tw])
+    tw = V("tt", T.fo[:], count, T.lp[:], A.add, deps=[tw], key="cw")
+    tx = V("tt", T.m2[:], T.m1[:, 0:32], T.m1[:, 32:64], A.max, deps=[tx], key="cx")
+    V("tt", T.g2[:], T.m1[:, 32:64], T.m1[:, 0:32], A.is_gt, key="cy")
+    t = V("ts", T.offa[:], T.fo[:], T.bt[:, 31:32], 1 / N, A.add, A.mult, deps=[t, tw])
+    ty = V("tt", T.n2[:], T.m1[:, 0:32], T.m1[:, 32:64], A.is_ge, key="cy")
+    V("tt", T.w3[:, 16:32], T.m2[:, 16:32], T.m2[:, 0:16], A.is_gt, deps=[tx], key="cx")
+    tx = V("tt", T.w3[:, 0:16], T.m2[:, 0:16], T.m2[:, 16:32], A.is_ge, key="cx")
     t = V("cp", T.inv[:, 0:WIN].indirect(T.offa[:, 0:16]), T.val[:], deps=[t])
-    t = V("scan", T.sel[:], T.a4[:], T.inv[:, 0:64], 0.0, A.add, A.min, deps=[t])
+    V("tt", T.w2[:, 32:64], T.w3[:], T.g2[:], A.mult, deps=[tx, ty], key="cx")
+    tx = V("tt", T.w2[:, 0:32], T.w3[:], T.n2[:], A.mult, key="cx")
+    t = V("scan", T.sel[:], T.a4[:], T.inv[:, 1:65], 0.0, A.add, A.min, deps=[t])
+    V("tt", T.win[:, 64:128], T.w2[:], T.g1[:], A.mult, deps=[tx, kg1], key="kwin")
     kob = V("ts", T.offb[:], T.sel[:, 3:64:4], pt, None, A.add, deps=[t], key="kob")
+    kwin = V("tt", T.win[:, 0:64], T.w2[:], T.n1[:], A.mult, deps=[kn1], key="kwin")
     kg = S(T.pk[:, 128:256], T.xb[:, 0:1024].indirect(T.offb[:, 8:16]), deps=[kob], key="kg")
+    kw2 = S(T.win2[:], T.win[:], deps=[kwin], key="kw2")
     t = V("cp", T.pk[:, 0:128], T.xb[:, 0:1024].indirect(T.offb[:, 0:8]), deps=[kob])
+    tx = V("scan", T.cum[:], T.rm[:], T.win[:], 0.0, A.mult, A.add, deps=[kwin], key="cx")
     kpk = V("q", T.pq[:, OWN:OWN + 128], T.pp[:, OWN:OWN + 128], T.pk[:], deps=[t, kg, kpz], key="kpk")
 
     oq, op = T.pq[:, OWN:OWN + 64].bitcast(dt.uint8), T.pp[:, OWN:OWN + 64]
@@ -326,23 +320,11 @@ def rank_program(g, core, T, topo):
         return S(T.res[:, 512 * h + a:512 * h + b], T.ps[:, 512 * bank:512 * bank + b - a], deps=[k], key=key)
     wait("t", ("kwq0", 1), ("kwq1", 1), kpsr, kpk)
     ma = [product(h, OWN, OWN + 128, h, "ma%d" % h, []) for h in range(8)]
-
-    t = V("tt", T.m1[:], T.st[:, 0:64], T.st[:, 64:128], A.max, deps=[kst])
-    V("tt", T.g1[:], T.st[:, 64:128], T.st[:, 0:64], A.is_gt, key="cw")
-    t = V("tt", T.m2[:], T.m1[:, 0:32], T.m1[:, 32:64], A.max, deps=[t])
-    tw = V("tt", T.g2[:], T.m1[:, 32:64], T.m1[:, 0:32], A.is_gt, key="cw")
-    V("tt", T.w3[:, 16:32], T.m2[:, 16:32], T.m2[:, 0:16], A.is_gt, deps=[t])
-    t = V("tt", T.w3[:, 0:16], T.m2[:, 0:16], T.m2[:, 16:32], A.is_ge)
-    t = V("tt", T.w2[:, 32:64], T.w3[:], T.g2[:], A.mult, deps=[t, tw])
-    t = V("tt", T.w2[:, 0:32], T.w3[:], T.w2[:, 32:64], A.subtract, deps=[t])
-    t = V("tt", T.win[:, 64:128], T.w2[:], T.g1[:], A.mult, deps=[t])
-    kwin = V("tt", T.win[:, 0:64], T.w2[:], T.win[:, 64:128], A.subtract, deps=[t], key="kwin")
     da = [drain(h, OWN, OWN + 64, h, "da%d" % h, ma[h]) for h in range(8)]
-    kw2 = S(T.win2[:], T.win[:], deps=[kwin], key="kw2")
-    t = V("scan", T.cum[:], T.rm[:], T.win[:], 0.0, A.mult, A.add, deps=[kwin])
-    t = V("tr", T.t2[:], T.cum[:], deps=[t])
-    t = V("scan", T.ts2[:, 1:128], T.t2[:, 0:127], T.rm[:, 1:128], 0.0, A.add, A.mult, deps=[t])
+
+    t = V("tr", T.t2[:], T.cum[:], deps=[tx])
     tw = V("tt", T.win2[:, 0:128:16], T.win2[:, 0:128:16], T.k8[:], A.add, deps=[kw2], key="cw")
+    t = V("scan", T.ts2[:, 1:128], T.t2[:, 0:127], T.rm[:, 1:128], 0.0, A.add, A.mult, deps=[t])
     t = V("tr", T.b2[:], T.ts2[:], deps=[t])
     t = V("tt", T.win2[:, 0:128:16], T.win2[:, 0:128:16], T.b2[:, 15:128:16], A.add, deps=[t, tw])
     t = V("scan", T.cu2[:], T.rm[:], T.win2[:], 0.0, A.mult, A.add, deps=[t])
@@ -356,13 +338,16 @@ def rank_program(g, core, T, topo):
     tw = V("cp", T.wi[:], T.x1[:, 0:16], key="cw")
     V("cp", T.t1[64:128, 0:32], T.t1[0:64, 0:32], deps=[t])
     t = V("cp", T.t1[0:64, 32:64], T.t1[64:128, 32:64])
-    kfr = V("tt", T.fr[:], T.x1[:, 0:16], T.wi[:], A.subtract, deps=[tw], key="kfr")
-    for e in range(2):
+    tw = V("tt", T.fr[:], T.x1[:, 0:16], T.wi[:], A.subtract, deps=[tw], key="cw")
+
+    def offsets(e, deps, key):
         for b in range(4):
             a = b // 2 * 2 + e
-            t = V("cp", T.off[32 * b:32 * b + 32, 64 * e:64 * e + 64], T.t1[32 * a:32 * a + 32, 0:64], deps=[t] if e + b == 0 else [])
-    toff = t
-    kwn = S(T.wnv[:], T.fr[:], deps=[kfr], key="kwn", scale=16.0)
+            k = V("cp", T.off[32 * b:32 * b + 32, 64 * e:64 * e + 64], T.t1[32 * a:32 * a + 32, 0:64],
+                  deps=deps if b == 0 else [], key=key)
+        return k
+    toff = [offsets(0, [t], "cv")]
+    kwn = V("ts", T.wnv[:], T.fr[:], 16.0, None, A.mult, deps=[tw], key="kwn")
     wait("g", ("loc", loc))
     wait("y", kwn, ("loc", loc))
     run("y", g.sync.dma_start(T.wn[:], T.wnv[:]), "lwn", 16)
@@ -372,6 +357,7 @@ def rank_program(g, core, T, topo):
     md = product(0, OWN // 2, OWN, 7, "md", [da[7]])
     mb += [product(h, 0, OWN, h, "mb%d" % h, [da[h]]) for h in range(1, 7)]
     dd = V("cp", T.res[:, OWN // 2:OWN], T.ps[:, 512 * 7:512 * 7 + OWN // 2], deps=[md], key="dd")
+    toff.append(offsets(1, [], "cx"))
     mb.append(product(7, 0, OWN, 7, "mb7", [dd]))
     db = [drain(h, 0, OWN // (2 if h == 0 else 1), h, "db%d" % h, mb[h]) for h in range(8)]
 
@@ -385,13 +371,14 @@ def rank_program(g, core, T, topo):
         for i in range(2):
             a, b = 128 * i, 128 * i + 128
             if h == 0:
-                acc[i] = V("cp", out[:, a:b], found(0, a, b), deps=[toff, da[0], db[0], dd], key="ky%d" % i)
+                acc[i] = V("cp", out[:, a:b], found(0, a, b), deps=[toff[0], da[0], db[0], dd], key="ky%d" % i)
             else:
-                acc[i] = V("tt", out[:, a:b], found(h, a, b), prev[:, a:b], A.add, deps=[acc[i], da[h], db[h]], key="ky%d" % i)
+                acc[i] = V("tt", out[:, a:b], found(h, a, b), prev[:, a:b], A.add,
+                           deps=[acc[i], da[h], db[h], toff[h // 2 % 2]], key="ky%d" % i)
     for i, q in enumerate(("y", "s")):
         wait(q, acc[i])
         run(q, Q[q][0].dma_start(T.y[:, 128 * i:128 * i + 128], out[:, 128 * i:128 * i + 128]), "ly", 16)
 
-    wait("g", ("ly", 32), ("lwn", 16))
-    g.wait_ge(T.sem.cv, total["cv"])
-    g.wait_ge(T.sem.cw, total["cw"])
+    for c in CHAINS:
+        g.wait_ge(T.sem[c], total[c])
+    wait("g", ("lwn", 16), ("ly", 32))

from concourse.bass import DstId, RemoteDMATransfer
from concourse.mybir import dt, AluOpType as A, ActivationFunctionType

N = 8
CODES = "float8_e4m3fn_x4"
ROW = 80
WIN = 130 * ROW
OWN = 64 * (N - 1)
BIG = 1.5 * 2.0 ** 26


def sb(kind, **cols):
    return {k: ("sbuf", [128, n], kind) for k, n in cols.items()}


SCRATCH = {"ps": ("psum", [128, 4096], "float32")}
SCRATCH.update(sb("bfloat16", xb=1024, usl=32, u16=16, zb=560, pk=512, wz=4096, zz=512))
SCRATCH.update(sb(CODES, zq=140, xq=384, wq=1024, pq=576, rq=64))
SCRATCH.update(sb("uint8", zp=140, xp=384, wp=1024, pp=576, rp=64))
SCRATCH.update(sb("int32", pi=1, pj=4, wi=16))
SCRATCH.update(sb("float32", pf=4, p4=1, c64=64, d64=32, msk=64, val=256, pc=16, k8=8))
SCRATCH.update(sb("bfloat16", rm=128, a4=64, z8=128))
SCRATCH.update(sb("float32", rsc=16, sm=64, s32=32, sc=128, lose=16, lp=16, fo=16, inv=WIN, sel=64))
SCRATCH.update(sb("bfloat16", fl=128, cs=136, tt=32, ts=32, bt=32))
SCRATCH.update(sb("uint16", uo=4, offa=16, offb=16, off=128))
SCRATCH.update(sb("bfloat16", win=128, cum=128, t2=128, ts2=128, b2=128))
SCRATCH.update(sb("float32", st=128, g1=64, n1=64, m1=64, g2=32, n2=32, m2=32, w3=32, w2=64, win2=128, cu2=128, pr=128, f64=64,
                  f32=32, x1=32, t1=64, fr=16, wnv=16, res=4096, ya=256, yb=256))
CHAINS = ["cv", "cw", "cx", "cy"]
SEMAPHORES = (CHAINS + ["loc", "cq", "rs0", "rs1", "rs2", "kc",
                        "lus", "lx", "lw0", "lw1", "lwn", "ly",
                        "kz", "kzz", "kzq", "kxp", "kxq", "ksc", "kps", "kpsr", "kio", "kio0", "kpz", "kst", "kob", "kg",
                        "kw0", "kw1", "kw7", "kwq0", "kwq1", "kg1", "kn1", "md", "dd",
                        "kpk", "kwn", "kwin", "kw2", "ky0", "ky1"]
              + ["%s%d" % (k, h) for k in ("ma", "da", "mb", "db", "sc") for h in range(8)])


def order(T, topo):
    a = [c for c in T.cores if c == T.cores[0] or topo.may_write(T.cores[0], c)]
    return [a, [c for c in T.cores if c not in a]]


def roads(core, T, topo):
    two = order(T, topo)
    own, far = two if core in two[0] else two[::-1]
    k = own.index(core)
    near = own[k + 1:] + own[:k]
    far = far[k:] + far[:k]
    free = [c for c in topo.cores_of(core) if c not in T.cores]
    cand = [c for c in free if all(topo.may_write(c, d) for d in far)]
    a = [c for c in cand if topo.die(c) != topo.die(core)]
    b = [c for c in cand if topo.die(c) == topo.die(core)]
    rest = [c for c in free if c not in cand and topo.die(c) != topo.die(core)]
    codes = {a[0]: far[0::2], b[0]: far[1::2]}
    planes = {a[1]: far[0::2], b[1]: far[1::2], rest[0]: near[:2], rest[1]: near[2:]}
    return {"near": near, "far": far, "codes": codes, "planes": planes, "scores": codes, "helpers": list(codes) + list(planes)}


def column(src, dst, T):
    return 64 * ((T.rank_of(src) - T.rank_of(dst) - 1) % N)


def seat(k):
    return 4 * (k % 2) + 2 * (k // 2 % 2) + k // 4


def bits(engines):
    return sum(1 << e for e in engines)


def write(g, core, dests, engines, src, dsts, sem, T, topo):
    i = []
    for d in dests:
        rid, pid = topo.addr(d, core)
        i.append(DstId(rid=rid, pnc=pid))
    g.remote_dma_fused([RemoteDMATransfer(dst_ids=i, dma_engine_mask=bits(engines), remote_sem=T.sem[sem],
                                          srcs=[src], dsts=dsts)], local_sem=T.sem.loc)
    return len(engines)


def engines_of(core, near, helper, topo):
    off, every = topo.engines(core, near), topo.engines(core, helper)
    return off, [e for e in every if e not in off], every


def whole(g, out, pattern, base, cm, sem):
    g.iota(out, pattern, base, cm, allow_small_or_imprecise_dtypes=True).then_inc(sem, 1)


def constant(g, which, boss, T):
    v, kio, cv = g.vector, T.sem.kio, T.sem.cv
    half, n = which % 2, 1
    if which // 2 == 0:
        out = T.pc[:, 8 * half:8 * half + 8]
        whole(g, out, [[N, 8]], N * (ROW + 1 + 8 * half), N * ROW, kio)
    elif which // 2 == 1:
        out = T.a4[:, 32 * half:32 * half + 32]
        whole(g, T.pi[:], [[0, 1]], 0, 1, cv)
        whole(g, T.d64[:], [[0, 8], [1, 4]], 0, 0, cv)
        v.wait_ge(cv, 2)
        v.tensor_scalar(T.pj[:, 0:1], T.pi[:], 2, 3, A.arith_shift_right, A.bitwise_and).then_inc(cv, 1)
        v.wait_ge(cv, 3)
        v.tensor_copy(T.pf[:, 0:1], T.pj[:, 0:1]).then_inc(cv, 1)
        v.wait_ge(cv, 4)
        v.tensor_scalar(out, T.d64[:], T.pf[:, 0:1], 2048.0, A.is_equal, A.mult).then_inc(kio, 1)
    else:
        out, n = T.k8[:, 4 * half:4 * half + 4], 4
        for k in range(4 * half, 4 * half + 4):
            v.memset(T.k8[:, k:k + 1], column(T.cores[seat(k)], boss, T) - 1 + seat(k) / 16).then_inc(kio, 1)
    g.wait_ge(kio, n)
    return out


def relay(g, core, boss, T, topo):
    r = roads(boss, T, topo)
    if core not in r["helpers"]:
        return
    p = sum(order(T, topo), []).index(boss)
    eng = topo.engines(core, r["near"][0])
    _, eon, every = engines_of(boss, r["near"][0], core, topo)
    c = constant(g, r["helpers"].index(core), boss, T)
    n = write(g, core, [boss], eng, c, [c], "kc", T, topo)
    if core in r["scores"]:
        g.wait_ge(T.sem.rs0, len(eon))
        d = r["scores"][core]
        n += write(g, core, d, eng, T.rsc[:], [T.sc[:, 16 * p:16 * p + 16]] * len(d), "sc%d" % p, T, topo)
    if core in r["codes"]:
        g.wait_ge(T.sem.rs1, len(every))
        d = r["codes"][core]
        to = [T.pq[:, column(boss, e, T):column(boss, e, T) + 64].bitcast(dt.uint8) for e in d]
        n += write(g, core, d, eng, T.rq[:].bitcast(dt.uint8), to, "cq", T, topo)
    else:
        g.wait_ge(T.sem.rs2, len(every))
        d = r["planes"][core]
        n += write(g, core, d, eng, T.rp[:], [T.pp[:, column(boss, e, T):column(boss, e, T) + 64] for e in d], "cq", T, topo)
    g.wait_ge(T.sem.loc, n)


def rank_program(g, core, T, topo):
    rank = T.rank_of(core)
    if rank is None:
        for boss in T.cores:
            if core in topo.cores_of(boss):
                relay(g, core, boss, T, topo)
        return
    road = roads(core, T, topo)
    near, far = road["near"], road["far"]
    pieces = sum(order(T, topo), [])
    mine = pieces.index(core)

    Q = {"v": [g.vector, "cv"], "s": [g.scalar, None], "t": [g.tensor, None], "g": [g, None], "y": [g.sync, None]}
    total = {}
    seen = {q: {} for q in Q}

    def wait(q, *deps):
        for d in deps:
            if d is None:
                continue
            sem, val = d
            if sem in CHAINS:
                val = total[sem]
            if seen[q].get(sem, 0) < val:
                Q[q][0].wait_ge(T.sem[sem], val)
                seen[q][sem] = val

    def run(q, ins, key=None, n=1):
        sem = key or Q[q][1]
        ins.then_inc(T.sem[sem], n)
        total[sem] = total.get(sem, 0) + n
        return (sem, total[sem])

    def V(name, *args, deps=(), key=None):
        wait("v", *deps)
        f = {"set": g.vector.memset, "cp": g.vector.tensor_copy, "tt": g.vector.tensor_tensor, "ts": g.vector.tensor_scalar,
             "scan": g.vector.tensor_tensor_scan, "tr": g.vector.transpose, "q": g.vector.quantize_mx}[name]
        return run("v", f(*args), key)

    def S(out, in_, deps=(), key=None, **line):
        wait("s", *deps)
        return run("s", g.scalar.activation(out, in_, ActivationFunctionType.Identity if line else ActivationFunctionType.Copy, **line), key)

    def iota(out, pattern, base, cm, key="kio"):
        return run("g", g.iota(out, pattern, base, cm, allow_small_or_imprecise_dtypes=True), key)

    lus = run("y", g.sync.dma_start(T.usl[:], T.us[:, 0:32]), "lus", 16)
    lx = run("s", g.scalar.dma_start(T.xb[:], T.x[:]), "lx", 16)

    iota(T.pi[:], [[0, 1]], 0, 1, "kio0")
    kio0 = iota(T.p4[:], [[0, 1]], 48, 4, "kio0")
    iota(T.c64[:], [[1, 4], [0, 16]], 0, 0)
    kio = iota(T.val[:], [[4, 16], [64, 16]], 0, 0)

    kzz = V("set", T.zz[:], 0.0, key="kzz")
    kz = V("set", T.zb[:], 0.0, key="kz")
    wait("v", kio0)
    V("ts", T.pj[:, 0:1], T.pi[:], 3, None, A.bitwise_and)
    V("ts", T.pj[:, 1:2], T.pi[:], 15, None, A.bitwise_and)
    t = V("ts", T.pj[:, 2:3], T.pi[:], 2, 28, A.arith_shift_right, A.bitwise_and)
    kxp = V("q", T.xq[:, 256:384], T.xp[:, 256:384], T.zz[:], deps=[kzz], key="kxp")
    tp = V("cp", T.pf[:, 0:1], T.pj[:, 0:1], deps=[t])
    pt = T.pf[:, 0:1]
    V("ts", T.uo[:, 2:3], T.pj[:, 1:2], -3.0, T.p4[:], A.mult, A.add)
    t = V("ts", T.uo[:, 0:1], T.pj[:, 2:3], pt, None, A.add, deps=[tp])

    def zero(block, key):
        return S(T.wz[:, 512 * block:512 * block + 512], T.zz[:], deps=[kzz], key=key)
    for h in range(7):
        zero(h, "kw0" if h < 4 else "kw1")
    t = V("cp", T.u16[:], T.usl[:, 0:32].indirect(T.uo[:, 0:1]), deps=[t, lus])
    t = V("cp", T.zb[:, 0:560].indirect(T.uo[:, 2:3]), T.u16[:], deps=[t, kz])
    kzq = V("q", T.zq[:], T.zp[:], T.zb[:], deps=[t], key="kzq")
    kxq = V("q", T.xq[:, 0:256], T.xp[:, 0:256], T.xb[:], deps=[lx], key="kxq")
    tm = V("ts", T.msk[:], T.c64[:], pt, None, A.is_equal, deps=[kio])
    kw7 = V("set", T.wz[:, 512 * 7:512 * 8], 0.0, key="kw7")

    wait("t", kzq, kxp, kxq)
    for i in range(4):
        m = g.tensor.matmul_mx(T.ps[:, 0:128], T.zq[:, 12 - 4 * i:140 - 4 * i], T.zp[:, 12 - 4 * i:140 - 4 * i],
                               T.xq[:, 64 * i:64 * i + 128], T.xp[:, 64 * i:64 * i + 128], i == 0, i == 3)
    kps = run("t", m, "kps")
    kpsr = V("tt", T.sm[:], T.ps[:, 0:64], T.msk[:], A.mult, deps=[kps, tm], key="kpsr")
    V("set", T.rm[:], 1.0, key="cw")
    V("set", T.z8[:], 0.0, key="cw")
    t = V("tt", T.s32[:], T.sm[:, 0:32], T.sm[:, 32:64], A.add, deps=[kpsr])
    V("set", T.ts[:, 0:1], 0.0, key="cw")
    tw = V("set", T.ts2[:, 0:1], 0.0, key="cw")
    own = T.sc[:, 16 * mine:16 * mine + 16]
    ksc = V("tt", own, T.s32[:, 0:16], T.s32[:, 16:32], A.add, deps=[t], key="ksc")

    hs = list(road["scores"])
    eoff, eon, every = engines_of(core, near[0], hs[0], topo)
    theirs = {c: roads(c, T, topo) for c in near + far}

    def arriving(c, *kinds):
        return sum(len(topo.engines(h, core)) for k in kinds for h, d in theirs[c][k].items() if core in d)
    landed = {c: ("sc%d" % pieces.index(c), len(eoff) if c in near else arriving(c, "scores")) for c in near + far}
    others = sorted(near, key=lambda c: theirs[c]["near"].index(core)) + sorted(far, key=lambda c: theirs[c]["far"].index(core))
    kc = ("kc", sum(len(topo.engines(h, near[0])) for h in road["helpers"]))
    wait("g", ksc)
    loc = write(g, core, hs, eon, own, [T.rsc[:]] * len(hs), "rs0", T, topo)
    loc += write(g, core, near, eoff, own, [own] * len(near), "sc%d" % mine, T, topo)

    for half, kw in enumerate(([("kw0", 4)], [("kw1", 3), kw7])):
        wait("y", *kw)
        for h in range(4 * half, 4 * half + 4):
            run("y", g.sync.dma_start(T.wz[16 * h:16 * h + 16, 512 * h:512 * h + 512], T.w[16 * h:16 * h + 16, :]), "lw%d" % half, 16)

    def wquant(half):
        V("q", T.wq[:, 512 * half:512 * half + 512], T.wp[:, 512 * half:512 * half + 512],
          T.wz[:, 2048 * half:2048 * half + 2048], deps=[("lw%d" % half, 64)], key="kwq%d" % half)

    kpz = S(T.pk[:, 256:512], T.zz[:, 0:256], deps=[kzz], key="kpz")
    V("set", T.inv[:, 0:ROW], 1020.0)
    V("set", T.cs[:, 0:N], 0.0)
    V("set", T.fl[:, N - 1:128:N], BIG)
    V("set", T.rm[:, 0:128:16], 0.0, deps=[tw])
    V("set", T.z8[:, 0:128:N], N / 2 + 0.5)
    V("set", T.z8[:, N - 1:128:N], BIG)
    wquant(0)
    wquant(1)

    def piece(c):
        return T.sc[:, 16 * pieces.index(c):16 * pieces.index(c) + 16]

    def seated(c, dep):
        a = 16 * [seat(k) for k in range(N)].index(T.rank_of(c))
        return S(T.st[:, a:a + 16], piece(c), deps=[dep], key="kst")

    def beaten(k, c, dep):
        return V("tt", T.fl[:, k:128:N], piece(c), own, A.is_ge if T.rank_of(c) < rank else A.is_gt, deps=[dep])
    seated(core, ksc)
    wait("v", ksc, kc)
    for k, c in enumerate(others):
        kst = seated(c, landed[c])
        t = beaten(k, c, landed[c])

    t = V("scan", T.cs[:, N:], T.z8[:], T.fl[:], 0.0, A.add, A.subtract, deps=[t])
    count = T.cs[:, 2 * N - 1::N]
    t = V("tr", T.tt[:], T.cs[:, 104:136], deps=[t])
    tw = V("tt", T.lose[:], count, T.cs[:, N - 1:128 + N - 1:N], A.is_equal, key="cw")
    tx = V("tt", T.m1[:], T.st[:, 0:64], T.st[:, 64:128], A.max, deps=[kst], key="cx")
    t = V("scan", T.ts[:, 1:32], T.tt[:, 0:31], T.rm[:, 1:32], 0.0, A.add, A.mult, deps=[t])
    tw = V("tt", T.lp[:], T.lose[:], T.pc[:], A.mult, deps=[tw], key="cw")
    kg1 = V("tt", T.g1[:], T.st[:, 64:128], T.st[:, 0:64], A.is_gt, key="kg1")
    kn1 = S(T.n1[:], T.g1[:], deps=[kg1], key="kn1", scale=-1.0, bias=1.0)
    t = V("tr", T.bt[:], T.ts[:], deps=[t])
    tw = V("tt", T.fo[:], count, T.lp[:], A.add, deps=[tw], key="cw")
    tx = V("tt", T.m2[:], T.m1[:, 0:32], T.m1[:, 32:64], A.max, deps=[tx], key="cx")
    V("tt", T.g2[:], T.m1[:, 32:64], T.m1[:, 0:32], A.is_gt, key="cy")
    t = V("ts", T.offa[:], T.fo[:], T.bt[:, 31:32], 1 / N, A.add, A.mult, deps=[t, tw])
    ty = V("tt", T.n2[:], T.m1[:, 0:32], T.m1[:, 32:64], A.is_ge, key="cy")
    V("tt", T.w3[:, 16:32], T.m2[:, 16:32], T.m2[:, 0:16], A.is_gt, deps=[tx], key="cx")
    tx = V("tt", T.w3[:, 0:16], T.m2[:, 0:16], T.m2[:, 16:32], A.is_ge, key="cx")
    t = V("cp", T.inv[:, 0:WIN].indirect(T.offa[:, 0:16]), T.val[:], deps=[t])
    V("tt", T.w2[:, 32:64], T.w3[:], T.g2[:], A.mult, deps=[tx, ty], key="cx")
    tx = V("tt", T.w2[:, 0:32], T.w3[:], T.n2[:], A.mult, key="cx")
    t = V("scan", T.sel[:], T.a4[:], T.inv[:, 1:65], 0.0, A.add, A.min, deps=[t])
    V("tt", T.win[:, 64:128], T.w2[:], T.g1[:], A.mult, deps=[tx, kg1], key="kwin")
    kob = V("ts", T.offb[:], T.sel[:, 3:64:4], pt, None, A.add, deps=[t], key="kob")
    kwin = V("tt", T.win[:, 0:64], T.w2[:], T.n1[:], A.mult, deps=[kn1], key="kwin")
    kg = S(T.pk[:, 128:256], T.xb[:, 0:1024].indirect(T.offb[:, 8:16]), deps=[kob], key="kg")
    kw2 = S(T.win2[:], T.win[:], deps=[kwin], key="kw2")
    t = V("cp", T.pk[:, 0:128], T.xb[:, 0:1024].indirect(T.offb[:, 0:8]), deps=[kob])
    tx = V("scan", T.cum[:], T.rm[:], T.win[:], 0.0, A.mult, A.add, deps=[kwin], key="cx")
    kpk = V("q", T.pq[:, OWN:OWN + 128], T.pp[:, OWN:OWN + 128], T.pk[:], deps=[t, kg, kpz], key="kpk")

    oq, op = T.pq[:, OWN:OWN + 64].bitcast(dt.uint8), T.pp[:, OWN:OWN + 64]
    wait("g", kpk)
    loc += write(g, core, list(road["codes"]), every, oq, [T.rq[:].bitcast(dt.uint8)] * len(road["codes"]), "rs1", T, topo)
    loc += write(g, core, list(road["planes"]), every, op, [T.rp[:]] * len(road["planes"]), "rs2", T, topo)
    loc += write(g, core, near, eoff, oq, [T.pq[:, column(core, c, T):column(core, c, T) + 64].bitcast(dt.uint8) for c in near],
                 "cq", T, topo)

    def product(h, a, b, bank, key, deps):
        wait("t", *deps)
        return run("t", g.tensor.matmul_mx(T.ps[:, 512 * bank:512 * bank + b - a], T.wq[:, 128 * h:128 * h + 128],
                                           T.wp[:, 128 * h:128 * h + 128], T.pq[:, a:b], T.pp[:, a:b], True, True), key)

    def drain(h, a, b, bank, key, k):
        return S(T.res[:, 512 * h + a:512 * h + b], T.ps[:, 512 * bank:512 * bank + b - a], deps=[k], key=key)
    wait("t", ("kwq0", 1), ("kwq1", 1), kpsr, kpk)
    ma = [product(h, OWN, OWN + 128, h, "ma%d" % h, []) for h in range(8)]
    da = [drain(h, OWN, OWN + 64, h, "da%d" % h, ma[h]) for h in range(8)]

    t = V("tr", T.t2[:], T.cum[:], deps=[tx])
    tw = V("tt", T.win2[:, 0:128:16], T.win2[:, 0:128:16], T.k8[:], A.add, deps=[kw2], key="cw")
    t = V("scan", T.ts2[:, 1:128], T.t2[:, 0:127], T.rm[:, 1:128], 0.0, A.add, A.mult, deps=[t])
    t = V("tr", T.b2[:], T.ts2[:], deps=[t])
    t = V("tt", T.win2[:, 0:128:16], T.win2[:, 0:128:16], T.b2[:, 15:128:16], A.add, deps=[t, tw])
    t = V("scan", T.cu2[:], T.rm[:], T.win2[:], 0.0, A.mult, A.add, deps=[t])
    t = V("tt", T.pr[:], T.cu2[:], T.win[:], A.mult, deps=[t])
    t = V("tt", T.f64[:], T.pr[:, 0:64], T.pr[:, 64:128], A.add, deps=[t])
    t = V("tt", T.f32[:], T.f64[:, 0:32], T.f64[:, 32:64], A.add, deps=[t])
    V("tt", T.x1[:, 0:16], T.f32[:, 0:16], T.f32[:, 16:32], A.add, deps=[t])
    t = V("tt", T.x1[:, 16:32], T.f32[:, 0:16], T.f32[:, 16:32], A.add)
    V("tr", T.t1[0:64, 0:32], T.x1[0:64, :], deps=[t])
    t = V("tr", T.t1[64:128, 32:64], T.x1[64:128, :])
    tw = V("cp", T.wi[:], T.x1[:, 0:16], key="cw")
    V("cp", T.t1[64:128, 0:32], T.t1[0:64, 0:32], deps=[t])
    t = V("cp", T.t1[0:64, 32:64], T.t1[64:128, 32:64])
    tw = V("tt", T.fr[:], T.x1[:, 0:16], T.wi[:], A.subtract, deps=[tw], key="cw")

    def offsets(e, deps, key):
        for b in range(4):
            a = b // 2 * 2 + e
            k = V("cp", T.off[32 * b:32 * b + 32, 64 * e:64 * e + 64], T.t1[32 * a:32 * a + 32, 0:64],
                  deps=deps if b == 0 else [], key=key)
        return k
    toff = [offsets(0, [t], "cv")]
    kwn = V("ts", T.wnv[:], T.fr[:], 16.0, None, A.mult, deps=[tw], key="kwn")
    wait("g", ("loc", loc))
    wait("y", kwn, ("loc", loc))
    run("y", g.sync.dma_start(T.wn[:], T.wnv[:]), "lwn", 16)

    wait("t", ("cq", sum(len(eoff) + arriving(c, "planes") for c in near) + sum(arriving(c, "codes", "planes") for c in far)))
    mb = [product(0, 0, OWN // 2, 0, "mb0", [da[0]])]
    md = product(0, OWN // 2, OWN, 7, "md", [da[7]])
    mb += [product(h, 0, OWN, h, "mb%d" % h, [da[h]]) for h in range(1, 7)]
    dd = V("cp", T.res[:, OWN // 2:OWN], T.ps[:, 512 * 7:512 * 7 + OWN // 2], deps=[md], key="dd")
    toff.append(offsets(1, [], "cx"))
    mb.append(product(7, 0, OWN, 7, "mb7", [dd]))
    db = [drain(h, 0, OWN // (2 if h == 0 else 1), h, "db%d" % h, mb[h]) for h in range(8)]

    def found(h, a, b):
        o = 64 * (h // 2 % 2) + 32 * (h // 4) + 16 * (h % 2)
        return T.res[:, 512 * h:512 * h + 512].indirect(T.off[:, o + a // 16:o + b // 16])
    out, prev = T.ya, T.yb
    acc = [None, None]
    for h in range(8):
        out, prev = prev, out
        for i in range(2):
            a, b = 128 * i, 128 * i + 128
            if h == 0:
                acc[i] = V("cp", out[:, a:b], found(0, a, b), deps=[toff[0], da[0], db[0], dd], key="ky%d" % i)
            else:
                acc[i] = V("tt", out[:, a:b], found(h, a, b), prev[:, a:b], A.add,
                           deps=[acc[i], da[h], db[h], toff[h // 2 % 2]], key="ky%d" % i)
    for i, q in enumerate(("y", "s")):
        wait(q, acc[i])
        run(q, Q[q][0].dma_start(T.y[:, 128 * i:128 * i + 128], out[:, 128 * i:128 * i + 128]), "ly", 16)

    for c in CHAINS:
        g.wait_ge(T.sem[c], total[c])
    wait("g", ("lwn", 16), ("ly", 32))
